import numpy as np
CORES = [11,27,43,59,75,91,107,123]
N = 8
T, K = 512, 2
ROUTE = [[[6,1],[1,2],[2,4],[5,1],[3,6],[3,6],[2,7],[3,4],[4,6],[2,5],[3,5],[6,5],[2,5],[3,2],[1,5],[6,2],[3,5],[1,6],[1,6],[2,0],[5,3],[0,5],[3,5],[7,5],[0,2],[5,4],[7,3],[2,1],[5,3],[0,7],[4,5],[6,2],[1,6],[3,1],[0,7],[7,4],[1,6],[7,0],[7,0],[2,0],[7,1],[5,4],[4,0],[7,3],[3,1],[0,4],[6,1],[2,6],[2,4],[2,5],[0,5],[2,5],[3,7],[0,7],[4,5],[3,2],[4,6],[0,2],[6,7],[1,2],[4,7],[7,4],[7,1],[7,4],[3,1],[1,3],[6,4],[6,1],[4,0],[4,6],[0,3],[4,2],[3,2],[7,4],[1,0],[6,0],[4,6],[5,6],[4,5],[1,5],[2,7],[7,1],[3,4],[6,5],[7,5],[3,4],[4,3],[2,4],[6,7],[1,3],[0,2],[7,0],[5,4],[4,3],[2,6],[3,4],[5,2],[7,6],[0,4],[2,6],[7,6],[4,6],[5,0],[5,4],[3,5],[2,4],[6,1],[1,0],[7,4],[1,2],[0,2],[0,1],[4,6],[7,0],[2,0],[5,7],[0,4],[5,0],[2,7],[0,6],[0,3],[2,4],[6,1],[6,5],[2,5],[3,4],[5,2],[6,2],[6,5],[3,4],[3,7],[7,3],[2,6],[5,4],[6,7],[7,3],[4,3],[7,5],[2,3],[5,3],[2,3],[3,2],[6,2],[2,7],[1,6],[1,4],[0,7],[4,0],[5,3],[5,7],[7,6],[1,7],[7,1],[1,4],[5,3],[0,1],[0,7],[3,2],[0,4],[3,0],[4,3],[4,1],[3,0],[5,2],[7,6],[1,2],[2,3],[1,3],[1,4],[5,6],[0,3],[7,0],[6,5],[6,2],[2,0],[2,3],[5,2],[7,3],[0,4],[7,3],[4,1],[4,2],[4,2],[6,0],[0,7],[4,3],[5,7],[4,5],[6,3],[0,2],[5,7],[4,7],[7,3],[4,2],[1,0],[0,7],[6,4],[2,3],[7,5],[7,4],[3,1],[2,6],[1,2],[5,0],[4,2],[1,7],[4,7],[0,1],[3,0],[0,6],[1,3],[4,3],[5,0],[3,7],[5,2],[5,3],[7,4],[5,1],[1,2],[1,7],[3,6],[0,5],[6,1],[6,7],[1,0],[0,7],[1,3],[7,3],[2,7],[6,7],[1,5],[5,3],[1,3],[6,5],[6,0],[4,5],[5,7],[5,2],[2,5],[0,3],[1,4],[6,5],[4,5],[0,5],[5,3],[0,7],[0,2],[0,7],[6,1],[7,6],[1,5],[1,4],[2,4],[1,0],[4,5],[4,3],[5,0],[7,2],[6,3],[7,6],[7,6],[6,1],[5,3],[3,0],[3,0],[2,0],[6,3],[5,1],[7,6],[6,1],[3,1],[4,6],[6,3],[1,3],[6,7],[1,0],[5,6],[2,0],[5,2],[2,5],[4,6],[6,1],[2,4],[6,1],[7,1],[2,0],[7,3],[5,3],[3,4],[3,4],[7,3],[0,2],[0,6],[4,5],[4,7],[0,3],[3,5],[6,7],[5,1],[1,6],[2,7],[6,7],[3,1],[5,2],[6,0],[4,1],[1,0],[2,1],[3,0],[3,4],[5,4],[2,1],[4,3],[5,0],[3,6],[3,0],[1,7],[6,0],[5,6],[6,7],[3,0],[4,7],[4,3],[1,0],[4,3],[1,2],[3,6],[1,3],[3,7],[6,4],[7,6],[7,6],[3,6],[0,6],[6,5],[6,0],[0,1],[4,3],[3,1],[3,4],[7,4],[7,6],[5,3],[7,6],[6,4],[5,4],[4,3],[6,5],[2,1],[4,2],[4,6],[2,6],[3,0],[0,7],[1,3],[3,2],[5,2],[1,3],[0,3],[5,1],[6,3],[1,3],[5,6],[5,1],[1,7],[3,6],[2,3],[4,6],[5,1],[7,1],[5,1],[2,6],[1,3],[6,0],[2,3],[3,7],[5,7],[2,3],[2,5],[4,5],[7,3],[3,1],[3,2],[0,1],[7,0],[3,1],[3,2],[7,1],[2,4],[0,5],[5,7],[6,7],[2,7],[1,3],[0,1],[3,4],[6,0],[5,2],[3,5],[6,3],[7,6],[7,4],[2,7],[5,1],[7,1],[0,4],[4,6],[5,1],[3,0],[0,1],[0,4],[3,6],[6,3],[1,0],[4,6],[1,4],[7,6],[2,4],[0,4],[3,7],[3,4],[2,7],[0,2],[4,3],[1,2],[5,3],[5,0],[1,7],[1,2],[2,3],[6,0],[6,4],[3,2],[5,7],[3,5],[5,3],[3,4],[5,0],[1,2],[0,3],[1,5],[4,0],[3,4],[7,1],[0,1],[3,4],[0,5],[1,7],[1,0],[4,0],[7,1],[6,4],[4,5],[1,4],[2,4],[2,0],[1,4],[3,1],[3,4],[7,1],[2,0],[4,1],[1,2],[6,0],[5,4],[3,7],[7,0],[5,1],[0,1],[1,3],[1,0],[0,2],[3,5],[6,2],[2,4],[1,3],[2,6],[5,3],[6,2],[6,2],[6,0],[7,3],[2,0],[0,5],[2,3],[2,1],[7,0],[5,7],[4,7],[6,7],[5,1],[4,6],[2,7],[3,4],[7,6],[3,2],[5,4],[4,1],[1,3],[3,5],[4,6],[1,5],[5,3],[4,5],[5,3],[0,3],[0,6],[4,3],[1,7],[1,3],[4,7],[0,4]],[[7,2],[2,6],[7,2],[2,0],[0,7],[1,6],[5,2],[0,3],[3,6],[0,7],[6,0],[3,5],[5,7],[6,1],[7,5],[6,1],[0,4],[7,5],[6,4],[4,3],[1,3],[7,4],[1,5],[4,0],[0,2],[7,0],[3,2],[0,6],[3,4],[6,5],[1,5],[0,3],[6,3],[5,3],[3,6],[2,4],[3,2],[0,2],[1,5],[3,4],[0,4],[0,4],[4,0],[3,0],[6,0],[7,2],[6,7],[0,4],[1,7],[3,5],[5,2],[0,7],[6,4],[3,4],[2,7],[4,1],[5,3],[1,2],[2,7],[2,7],[6,1],[7,2],[7,0],[7,6],[3,5],[5,4],[4,5],[1,5],[6,7],[1,7],[2,0],[2,4],[1,2],[6,4],[0,1],[0,1],[0,1],[3,2],[2,4],[5,0],[3,6],[2,3],[5,7],[2,4],[4,6],[6,2],[5,1],[4,3],[5,6],[4,3],[5,0],[4,2],[6,4],[5,0],[2,0],[7,1],[6,4],[1,0],[1,0],[4,1],[0,6],[3,6],[1,6],[6,1],[5,2],[1,7],[4,6],[0,2],[0,3],[6,5],[6,7],[7,5],[0,5],[7,3],[2,0],[1,2],[1,6],[6,2],[5,4],[7,1],[2,7],[3,7],[5,3],[4,1],[1,0],[5,2],[3,1],[7,1],[2,7],[1,0],[2,3],[3,6],[1,5],[2,1],[3,1],[5,0],[0,6],[3,5],[6,5],[1,5],[0,6],[2,4],[7,1],[0,5],[1,3],[0,5],[2,4],[5,0],[3,5],[0,6],[7,1],[0,4],[0,6],[0,3],[6,1],[5,1],[6,4],[4,1],[0,2],[2,0],[5,4],[5,4],[4,2],[4,7],[4,5],[5,1],[4,7],[4,7],[0,4],[2,1],[4,0],[7,5],[1,0],[6,5],[0,5],[1,2],[2,1],[0,1],[5,3],[2,0],[2,1],[7,5],[1,7],[3,5],[0,6],[3,0],[6,7],[7,1],[6,3],[0,5],[5,3],[1,6],[3,1],[1,2],[5,0],[4,1],[2,4],[6,3],[5,6],[5,7],[1,6],[1,5],[0,7],[1,2],[2,0],[4,5],[3,1],[7,6],[7,1],[5,2],[1,0],[6,0],[1,7],[0,6],[6,3],[0,4],[0,6],[6,5],[3,1],[0,5],[2,6],[5,6],[2,6],[6,3],[1,2],[7,0],[5,3],[1,6],[3,7],[7,1],[6,7],[4,3],[2,3],[6,3],[7,2],[3,2],[7,1],[3,7],[3,7],[1,7],[6,4],[2,1],[1,3],[0,2],[5,3],[2,5],[2,5],[3,4],[6,5],[2,7],[3,0],[5,2],[6,5],[6,7],[3,0],[4,2],[3,4],[4,2],[4,3],[3,5],[4,3],[3,5],[5,4],[0,2],[5,1],[3,0],[3,6],[7,2],[0,7],[7,4],[5,2],[5,6],[6,4],[7,0],[4,7],[2,0],[4,3],[5,4],[4,3],[1,4],[1,4],[1,2],[3,4],[2,0],[1,5],[7,4],[2,3],[3,6],[4,2],[2,6],[2,1],[2,5],[2,7],[0,2],[7,4],[2,0],[5,3],[2,3],[1,4],[1,0],[7,3],[7,3],[5,4],[2,6],[3,1],[5,6],[3,2],[4,3],[4,2],[5,3],[0,1],[6,3],[0,1],[4,2],[2,4],[4,3],[5,1],[0,6],[0,6],[3,7],[0,1],[4,3],[6,7],[6,5],[1,7],[4,0],[7,5],[3,6],[2,3],[7,4],[5,7],[2,1],[2,0],[2,0],[2,4],[1,0],[7,3],[5,3],[0,6],[3,1],[1,7],[3,0],[7,5],[3,1],[2,5],[6,3],[2,7],[5,4],[4,7],[4,1],[4,1],[2,0],[1,7],[7,6],[7,1],[7,1],[2,7],[4,0],[5,1],[0,7],[7,3],[7,4],[5,0],[5,4],[4,5],[5,0],[2,5],[6,7],[3,4],[6,1],[6,0],[3,2],[3,0],[5,1],[1,7],[2,7],[1,2],[7,2],[7,5],[5,4],[7,1],[3,1],[0,7],[6,5],[7,4],[6,7],[1,3],[4,7],[6,2],[6,2],[1,4],[2,6],[3,6],[3,2],[4,7],[4,1],[7,4],[1,7],[6,7],[5,6],[4,0],[5,7],[5,6],[4,5],[2,3],[2,4],[1,6],[3,2],[6,5],[5,3],[2,0],[7,5],[1,7],[1,0],[1,2],[2,3],[7,0],[3,0],[0,4],[2,3],[6,1],[4,6],[2,3],[0,5],[5,7],[6,0],[0,6],[1,5],[5,2],[7,0],[6,0],[3,5],[3,7],[2,3],[0,5],[3,5],[2,3],[7,0],[6,3],[7,6],[5,2],[1,7],[7,4],[2,7],[7,3],[0,2],[4,1],[6,4],[3,7],[5,6],[6,2],[6,5],[2,7],[3,2],[6,7],[0,5],[3,2],[3,1],[2,6],[2,4],[0,5],[0,6],[2,6],[5,6],[7,2],[4,1],[4,6],[0,5],[2,4],[1,7],[5,7],[2,7],[5,0],[1,5],[1,0],[2,4],[0,4],[1,4],[6,7],[1,6],[3,4],[3,0],[3,7],[3,7],[6,7],[1,5],[5,2],[6,1],[3,2],[0,3],[2,6],[2,6],[6,1],[0,4],[7,2],[2,1],[4,3],[2,6],[6,3],[1,5],[7,3],[3,5],[1,6],[6,5],[2,3],[3,4],[5,3],[5,2],[2,5],[6,1],[1,5],[2,1]],[[0,6],[7,1],[2,7],[5,4],[0,6],[5,3],[7,4],[4,0],[2,3],[5,6],[4,1],[1,7],[4,5],[3,7],[5,7],[4,3],[3,7],[2,4],[5,7],[3,2],[0,6],[6,5],[2,5],[2,3],[0,7],[5,0],[5,3],[4,6],[0,2],[0,1],[5,1],[6,2],[3,7],[1,0],[4,5],[7,6],[0,7],[6,3],[4,0],[2,4],[0,7],[2,4],[5,4],[7,1],[0,4],[4,6],[0,4],[7,0],[6,4],[2,4],[4,5],[3,0],[3,2],[6,1],[6,4],[2,4],[1,6],[7,0],[5,7],[4,6],[2,1],[3,5],[3,2],[6,2],[3,1],[1,4],[5,7],[2,1],[7,1],[7,0],[4,6],[3,7],[5,7],[2,7],[6,2],[7,5],[0,3],[3,1],[6,0],[6,0],[6,7],[7,1],[0,1],[6,3],[7,2],[1,4],[4,6],[6,5],[5,6],[2,5],[2,1],[6,0],[1,7],[1,4],[1,6],[2,6],[5,4],[6,0],[6,3],[3,4],[3,2],[0,2],[5,1],[5,0],[1,6],[0,1],[6,4],[7,5],[1,6],[1,0],[0,4],[7,5],[2,6],[6,2],[0,5],[5,1],[5,2],[4,7],[7,3],[2,3],[4,2],[3,2],[0,2],[7,3],[4,3],[1,4],[5,0],[6,1],[6,7],[0,3],[3,6],[4,2],[3,0],[5,7],[4,3],[1,6],[7,0],[2,4],[0,7],[4,6],[7,3],[5,0],[2,3],[7,1],[3,6],[1,6],[6,4],[6,0],[3,4],[1,4],[5,6],[1,3],[6,3],[0,1],[7,2],[4,5],[7,5],[5,3],[7,1],[0,6],[4,2],[5,7],[3,7],[3,1],[1,6],[4,6],[7,1],[0,6],[2,4],[7,3],[1,4],[2,4],[5,0],[2,0],[1,2],[2,7],[2,3],[2,7],[1,6],[3,0],[7,6],[6,0],[5,6],[0,2],[5,6],[5,7],[6,2],[0,5],[2,0],[7,0],[7,2],[4,3],[1,6],[5,4],[6,7],[3,2],[2,6],[6,1],[0,1],[6,3],[1,2],[3,4],[1,5],[3,2],[2,0],[5,0],[1,4],[6,2],[2,4],[5,7],[6,4],[2,6],[6,0],[6,2],[4,6],[7,6],[7,6],[5,4],[5,6],[6,0],[6,3],[4,1],[2,1],[6,0],[7,5],[1,2],[1,2],[1,5],[3,4],[0,7],[1,0],[0,1],[7,6],[0,2],[4,5],[6,4],[4,3],[0,6],[3,4],[0,7],[0,7],[4,7],[0,6],[3,2],[1,5],[7,1],[4,1],[1,5],[7,1],[1,2],[3,4],[0,2],[0,7],[1,2],[6,4],[3,4],[1,6],[4,6],[6,4],[4,1],[2,1],[4,0],[1,3],[6,0],[6,7],[0,5],[0,6],[6,5],[7,2],[6,1],[2,0],[6,2],[1,3],[7,0],[2,3],[3,6],[5,1],[2,7],[3,1],[1,0],[6,7],[6,3],[6,2],[5,7],[6,0],[0,6],[3,5],[1,2],[2,4],[6,0],[7,2],[6,4],[6,3],[6,5],[7,1],[7,4],[5,2],[3,4],[5,7],[6,4],[3,4],[1,0],[1,0],[6,3],[0,3],[0,4],[7,2],[7,2],[3,7],[2,3],[6,2],[2,0],[1,4],[4,6],[7,2],[4,7],[6,2],[5,1],[1,4],[7,1],[3,7],[2,1],[1,3],[5,4],[4,1],[4,6],[2,5],[6,1],[4,1],[0,2],[4,2],[4,0],[7,2],[3,1],[0,4],[3,7],[3,5],[1,0],[7,2],[7,5],[7,3],[2,1],[2,4],[6,0],[3,7],[1,7],[0,3],[0,4],[5,2],[6,7],[7,6],[7,3],[5,0],[2,5],[6,1],[1,4],[3,0],[4,2],[6,5],[1,7],[7,1],[6,4],[5,2],[6,3],[3,7],[7,1],[3,1],[2,1],[6,5],[2,1],[2,6],[6,2],[5,1],[5,0],[1,7],[2,0],[2,3],[3,6],[3,5],[0,1],[5,2],[2,6],[5,6],[7,2],[3,5],[7,6],[1,2],[6,2],[4,2],[2,1],[7,2],[0,3],[3,1],[0,5],[1,5],[5,0],[0,4],[6,3],[4,0],[0,3],[0,3],[5,2],[7,3],[5,1],[6,7],[0,6],[1,0],[7,2],[1,2],[4,7],[7,6],[0,2],[6,4],[2,6],[6,0],[2,1],[2,1],[7,5],[6,3],[4,5],[4,5],[7,6],[2,4],[4,1],[3,2],[3,6],[4,6],[0,5],[5,1],[6,7],[5,6],[7,2],[1,2],[4,5],[5,2],[1,3],[3,4],[3,1],[5,3],[2,0],[1,0],[4,2],[5,7],[5,4],[3,2],[2,6],[0,2],[2,6],[0,7],[1,2],[7,1],[0,1],[7,0],[1,5],[0,5],[3,5],[3,1],[0,7],[7,5],[7,6],[0,7],[1,6],[2,0],[2,1],[2,3],[5,3],[0,6],[2,6],[3,0],[6,1],[6,3],[6,7],[7,1],[3,1],[3,6],[5,7],[1,6],[6,5],[2,3],[6,0],[3,1],[4,0],[1,2],[5,2],[0,7],[4,3],[3,4],[3,0],[0,6],[1,2],[0,1],[0,6],[5,7],[7,4],[2,5],[3,2],[7,3],[5,0],[0,3],[1,4],[7,4],[4,3],[0,6],[5,2],[2,0],[7,6],[7,0],[0,4],[4,6],[0,2],[7,2],[1,3]],[[0,1],[2,3],[6,0],[6,7],[3,4],[3,5],[2,5],[1,6],[1,2],[3,1],[1,0],[0,2],[7,1],[1,7],[6,4],[5,7],[3,2],[3,5],[0,2],[4,6],[0,5],[5,4],[3,0],[4,6],[7,4],[3,1],[3,5],[2,3],[3,7],[7,2],[6,1],[2,1],[2,5],[1,2],[1,4],[4,2],[6,0],[4,3],[4,6],[5,4],[4,3],[6,3],[7,2],[5,6],[5,6],[1,6],[3,0],[1,3],[5,0],[4,6],[0,7],[7,4],[7,5],[3,4],[5,0],[5,0],[7,6],[5,0],[7,1],[1,2],[6,3],[7,2],[5,1],[6,1],[3,6],[5,0],[7,4],[6,3],[1,3],[3,0],[0,1],[7,0],[6,2],[3,4],[7,2],[2,0],[5,4],[0,5],[3,7],[4,7],[2,1],[1,3],[7,6],[2,0],[7,5],[2,6],[6,7],[1,2],[1,0],[4,5],[4,5],[3,2],[0,3],[2,5],[6,0],[4,5],[6,7],[2,0],[6,2],[3,7],[3,6],[6,4],[0,3],[2,6],[6,0],[1,7],[4,2],[0,4],[4,6],[4,0],[7,1],[4,1],[7,4],[4,5],[0,3],[2,5],[7,1],[1,4],[1,7],[3,0],[4,1],[5,4],[3,4],[3,0],[6,1],[4,0],[5,4],[0,1],[2,1],[7,0],[6,2],[0,5],[5,7],[2,0],[7,0],[4,1],[1,5],[5,0],[5,1],[6,2],[4,7],[5,3],[0,7],[4,5],[1,2],[7,4],[6,2],[5,3],[2,4],[2,7],[4,3],[7,2],[5,4],[2,3],[0,4],[3,7],[0,4],[6,5],[3,2],[4,3],[3,2],[7,1],[7,0],[0,5],[3,1],[6,4],[5,1],[4,6],[4,2],[7,2],[6,1],[6,2],[2,6],[7,0],[5,4],[1,4],[3,5],[6,2],[1,6],[7,1],[4,7],[1,4],[4,7],[5,3],[0,5],[7,5],[6,7],[4,2],[6,4],[5,3],[7,5],[1,6],[2,1],[0,2],[4,6],[4,6],[0,1],[0,6],[6,4],[6,1],[4,3],[4,0],[3,4],[0,6],[6,0],[0,2],[7,0],[3,0],[1,5],[3,1],[5,0],[5,0],[4,5],[7,0],[5,0],[6,4],[7,4],[4,0],[2,4],[2,3],[1,4],[6,2],[5,3],[4,3],[2,7],[1,3],[2,3],[1,7],[6,5],[1,4],[4,7],[1,4],[2,0],[4,3],[3,1],[4,6],[6,5],[4,1],[1,6],[4,0],[4,1],[5,4],[6,0],[4,7],[3,0],[3,0],[7,4],[5,0],[6,1],[3,7],[6,0],[6,2],[7,3],[2,7],[0,3],[6,3],[7,5],[3,6],[2,0],[4,5],[6,4],[4,0],[2,7],[5,4],[0,1],[1,6],[1,0],[3,0],[3,2],[2,0],[6,3],[2,4],[3,0],[1,3],[3,4],[2,1],[5,0],[1,5],[5,6],[3,1],[2,7],[6,2],[3,4],[6,0],[6,3],[1,2],[4,5],[2,6],[3,1],[4,6],[6,0],[4,7],[4,6],[1,5],[7,5],[1,3],[1,2],[7,4],[7,2],[4,3],[0,6],[6,0],[1,4],[5,1],[1,2],[6,1],[1,5],[5,7],[7,0],[2,6],[4,1],[2,3],[0,7],[6,5],[7,2],[7,4],[2,0],[7,4],[4,1],[4,1],[4,6],[3,5],[0,2],[3,0],[5,1],[7,3],[6,5],[3,2],[5,1],[4,3],[1,6],[7,6],[3,2],[0,1],[4,7],[1,7],[2,7],[4,0],[1,4],[3,2],[7,6],[2,3],[1,5],[2,6],[3,0],[1,4],[2,5],[0,5],[1,6],[6,5],[0,2],[0,7],[1,3],[7,3],[3,5],[6,5],[6,3],[5,6],[3,5],[1,4],[1,0],[5,1],[0,2],[4,1],[1,3],[4,5],[7,0],[1,3],[5,4],[6,2],[7,4],[2,7],[1,4],[6,4],[3,1],[2,5],[4,0],[2,0],[7,1],[1,5],[7,5],[1,7],[6,5],[7,3],[2,7],[4,1],[4,0],[2,0],[7,2],[7,0],[3,4],[3,2],[6,3],[1,2],[7,3],[3,0],[5,3],[0,4],[6,1],[1,5],[5,1],[7,1],[6,7],[6,2],[2,1],[2,4],[2,5],[2,1],[5,4],[0,4],[5,2],[0,3],[5,4],[7,2],[4,2],[6,0],[3,1],[1,3],[5,2],[4,7],[0,7],[7,6],[5,4],[2,4],[6,1],[2,6],[2,1],[4,0],[2,6],[6,1],[1,6],[2,1],[6,5],[2,5],[7,2],[5,6],[2,4],[4,2],[3,6],[2,5],[5,3],[1,3],[0,4],[4,3],[3,4],[6,0],[6,0],[0,4],[7,2],[4,3],[6,7],[0,4],[3,6],[5,2],[1,6],[2,6],[0,7],[6,0],[1,3],[5,1],[2,3],[0,5],[4,0],[1,7],[5,0],[4,7],[4,7],[7,6],[6,0],[6,0],[0,7],[6,0],[4,3],[5,2],[3,6],[2,7],[1,6],[6,3],[5,4],[5,6],[2,6],[4,7],[7,5],[0,4],[3,6],[5,2],[1,7],[7,1],[7,0],[4,5],[1,7],[7,5],[0,5],[4,6],[2,0],[7,1],[2,4],[6,2],[3,1],[6,5],[7,1],[2,5],[2,7],[4,1],[5,7],[6,2],[2,3],[1,7],[0,1],[0,2],[0,7],[3,5]],[[4,2],[2,1],[0,7],[7,1],[5,1],[2,3],[2,0],[7,1],[4,5],[7,2],[3,4],[7,0],[6,1],[7,5],[5,7],[6,3],[1,5],[6,0],[5,1],[0,3],[2,0],[7,6],[2,3],[2,5],[3,7],[5,3],[1,3],[6,2],[3,4],[4,3],[0,2],[3,4],[0,3],[7,1],[6,4],[3,2],[2,7],[3,4],[5,4],[2,3],[2,1],[6,7],[4,5],[3,2],[1,2],[6,1],[1,3],[2,4],[3,6],[4,3],[3,6],[5,0],[4,5],[6,2],[5,6],[1,6],[6,3],[0,1],[0,2],[3,5],[7,1],[3,4],[0,3],[3,5],[4,3],[4,3],[4,6],[1,5],[5,0],[5,3],[2,7],[2,5],[1,0],[3,7],[1,0],[0,5],[0,1],[1,7],[4,0],[6,3],[1,2],[2,1],[0,7],[6,5],[2,3],[1,4],[0,3],[4,0],[0,1],[5,4],[4,1],[3,6],[4,0],[5,2],[4,7],[2,7],[3,7],[6,5],[3,1],[0,3],[2,5],[1,4],[3,6],[2,1],[1,4],[4,5],[6,7],[4,6],[4,1],[7,0],[5,1],[3,5],[4,7],[5,4],[6,3],[5,3],[2,3],[4,0],[2,4],[5,6],[0,5],[7,6],[2,5],[0,2],[5,1],[3,1],[5,0],[4,0],[6,3],[0,1],[2,0],[5,4],[6,3],[6,1],[3,2],[1,0],[7,0],[3,5],[6,2],[5,4],[3,7],[0,4],[5,0],[7,1],[4,6],[5,4],[7,1],[7,3],[2,4],[0,2],[4,0],[1,5],[1,7],[0,6],[4,2],[0,2],[6,0],[1,3],[5,6],[1,3],[5,3],[4,7],[4,0],[2,7],[3,0],[5,3],[1,6],[1,6],[2,1],[6,5],[6,1],[5,6],[3,0],[4,2],[4,0],[3,4],[1,6],[4,2],[0,3],[0,2],[1,2],[7,2],[1,7],[7,6],[4,6],[2,0],[6,2],[5,1],[7,6],[0,5],[6,0],[2,0],[1,3],[4,7],[7,2],[4,6],[3,5],[0,3],[7,6],[7,6],[3,1],[2,6],[7,3],[1,6],[2,5],[0,4],[0,7],[4,3],[1,3],[3,4],[2,5],[5,4],[1,6],[2,1],[2,5],[5,6],[0,3],[1,7],[0,6],[6,4],[3,7],[6,5],[1,7],[5,2],[3,2],[4,3],[2,0],[1,4],[3,0],[4,2],[4,0],[6,2],[3,2],[0,1],[0,3],[5,6],[6,7],[6,2],[6,2],[7,3],[7,0],[6,2],[0,4],[6,7],[5,7],[2,1],[5,2],[3,5],[3,6],[0,4],[5,6],[7,6],[5,2],[3,6],[5,4],[7,5],[5,1],[6,1],[2,0],[1,4],[5,7],[1,0],[5,4],[4,3],[7,4],[4,0],[2,5],[2,1],[4,2],[3,5],[3,5],[6,3],[7,1],[1,7],[6,5],[0,1],[7,5],[2,0],[4,3],[2,0],[4,3],[3,7],[4,0],[0,2],[4,5],[3,2],[3,4],[4,2],[2,3],[2,3],[5,0],[5,2],[1,4],[7,6],[2,7],[3,4],[5,3],[2,6],[3,7],[1,3],[1,7],[1,0],[3,1],[1,4],[4,1],[0,5],[2,1],[6,5],[3,6],[3,2],[6,5],[5,1],[6,3],[2,4],[3,0],[3,6],[4,2],[7,3],[5,0],[2,1],[3,1],[6,3],[3,0],[4,3],[0,5],[0,5],[0,5],[0,2],[7,6],[5,0],[6,7],[7,3],[4,7],[6,0],[5,3],[0,7],[5,2],[3,0],[0,2],[2,1],[5,1],[2,7],[4,3],[4,6],[6,4],[6,4],[5,3],[0,1],[0,1],[4,0],[2,5],[3,4],[6,2],[5,1],[1,4],[5,0],[2,7],[0,1],[7,0],[5,3],[6,4],[3,0],[3,7],[1,4],[5,7],[4,3],[6,2],[1,4],[3,4],[7,0],[6,2],[3,5],[0,4],[6,4],[0,1],[7,6],[0,3],[2,0],[3,7],[4,2],[6,4],[3,0],[7,2],[0,3],[6,7],[1,4],[1,4],[5,0],[3,4],[5,7],[4,1],[0,5],[4,3],[0,6],[4,7],[7,5],[6,5],[7,0],[5,6],[4,5],[6,1],[0,2],[4,1],[3,1],[2,5],[4,3],[6,5],[3,5],[3,1],[7,2],[4,7],[5,7],[0,2],[0,3],[2,5],[0,5],[4,5],[3,5],[0,7],[0,6],[4,6],[0,1],[6,2],[4,5],[0,5],[4,0],[2,1],[0,1],[4,0],[7,4],[2,1],[5,7],[5,3],[0,6],[6,5],[4,0],[6,3],[0,5],[2,3],[6,5],[3,6],[2,0],[1,6],[1,6],[2,3],[0,3],[1,4],[7,3],[3,4],[3,4],[3,2],[7,0],[6,3],[4,5],[6,7],[4,5],[7,3],[4,5],[6,5],[1,6],[3,5],[2,7],[6,5],[2,4],[6,5],[0,6],[7,1],[1,4],[2,0],[2,6],[4,3],[6,0],[3,7],[2,7],[7,2],[1,6],[2,0],[4,2],[4,2],[3,6],[1,7],[5,2],[3,6],[7,4],[5,3],[6,5],[7,1],[0,6],[2,0],[1,0],[7,3],[3,4],[2,3],[5,4],[7,6],[2,4],[0,5],[7,1],[6,7],[2,0],[7,5],[5,7],[4,6],[5,4],[6,2],[7,3],[1,2],[2,6],[0,4],[7,3],[0,1],[1,3]],[[2,5],[2,6],[5,6],[2,3],[0,4],[0,3],[6,5],[2,0],[4,7],[7,5],[5,0],[2,5],[7,2],[5,7],[0,4],[3,1],[0,5],[2,0],[5,7],[5,6],[7,0],[3,4],[5,6],[2,3],[4,1],[7,5],[2,0],[7,3],[5,2],[5,7],[3,6],[6,0],[0,4],[5,1],[5,2],[7,5],[6,1],[2,0],[6,5],[0,5],[7,2],[7,6],[4,0],[3,7],[0,5],[7,3],[6,2],[6,3],[0,5],[6,2],[2,7],[6,1],[3,5],[4,2],[5,2],[3,6],[3,0],[1,0],[5,6],[5,3],[7,1],[6,2],[5,7],[3,5],[0,4],[6,0],[7,0],[2,6],[1,7],[6,2],[6,4],[2,3],[4,2],[1,0],[3,0],[3,6],[5,4],[4,6],[4,5],[6,5],[7,6],[2,7],[4,0],[0,2],[1,3],[3,2],[1,3],[6,3],[4,5],[3,1],[7,5],[2,5],[7,3],[7,3],[4,7],[7,1],[7,4],[3,5],[7,6],[5,1],[7,3],[3,2],[6,3],[6,4],[1,2],[5,3],[2,3],[4,7],[1,4],[6,0],[3,0],[4,1],[5,3],[4,3],[2,7],[7,0],[0,7],[0,4],[6,3],[7,0],[6,0],[2,1],[3,0],[4,1],[6,2],[4,6],[5,1],[2,7],[5,0],[3,2],[4,0],[7,0],[4,3],[3,7],[0,3],[3,5],[4,1],[7,5],[4,6],[6,2],[1,7],[5,0],[2,5],[2,5],[3,7],[0,6],[3,6],[0,2],[3,7],[3,7],[0,1],[1,3],[2,4],[1,7],[0,4],[2,1],[7,1],[5,2],[7,1],[4,6],[0,3],[0,6],[5,3],[4,6],[3,0],[5,6],[6,3],[6,5],[1,5],[0,5],[4,6],[2,3],[2,3],[4,3],[4,0],[6,0],[7,0],[3,4],[7,3],[6,5],[0,1],[7,0],[2,1],[7,2],[6,4],[3,5],[0,7],[4,1],[0,3],[6,0],[3,7],[1,2],[4,7],[7,3],[6,4],[2,6],[6,4],[4,1],[3,7],[6,2],[5,0],[3,6],[4,3],[7,5],[4,5],[7,6],[7,1],[0,4],[6,7],[1,0],[5,1],[2,1],[5,0],[6,1],[7,2],[3,1],[5,6],[4,3],[7,3],[6,5],[3,1],[4,5],[1,7],[5,3],[1,7],[3,1],[0,2],[5,0],[3,1],[0,2],[3,2],[3,4],[1,7],[7,3],[5,7],[4,0],[4,2],[7,3],[2,3],[5,2],[2,1],[5,4],[4,2],[1,4],[4,7],[0,5],[1,7],[2,3],[0,5],[0,3],[7,3],[0,1],[7,0],[0,3],[7,3],[0,2],[0,4],[4,5],[4,6],[0,4],[0,7],[3,6],[1,0],[6,5],[4,1],[6,3],[0,7],[4,5],[1,4],[5,7],[6,1],[7,3],[7,1],[7,2],[7,1],[7,2],[2,1],[6,1],[4,2],[5,6],[6,1],[5,7],[2,3],[7,0],[6,1],[0,4],[1,2],[4,5],[0,1],[6,4],[4,6],[1,6],[4,2],[7,1],[6,7],[5,6],[7,6],[2,6],[0,7],[1,7],[0,5],[3,0],[0,7],[4,1],[2,7],[4,0],[6,3],[2,4],[3,7],[6,2],[0,6],[7,3],[6,1],[6,4],[2,3],[1,2],[7,0],[6,1],[1,3],[0,3],[5,2],[3,6],[5,3],[0,5],[3,7],[7,1],[1,0],[1,2],[3,2],[4,3],[1,0],[2,3],[0,2],[3,2],[5,3],[4,5],[3,1],[7,5],[5,3],[1,2],[1,5],[3,4],[4,2],[5,0],[1,7],[4,5],[2,3],[4,2],[6,7],[6,5],[1,0],[1,6],[2,3],[2,5],[4,3],[4,7],[1,7],[5,4],[7,2],[5,4],[4,5],[2,4],[7,0],[2,5],[2,7],[7,3],[3,1],[1,6],[7,3],[1,6],[2,0],[7,5],[0,7],[2,7],[7,4],[1,7],[0,5],[4,6],[6,5],[4,0],[3,6],[3,6],[3,2],[0,5],[2,6],[3,7],[4,0],[6,4],[5,4],[0,3],[6,7],[6,7],[4,3],[5,7],[5,3],[4,5],[6,0],[3,1],[3,0],[1,2],[6,0],[6,3],[2,3],[1,5],[3,6],[2,1],[4,3],[6,7],[7,1],[0,3],[0,2],[0,2],[2,3],[7,1],[1,4],[6,0],[0,4],[1,3],[2,1],[2,6],[4,6],[1,7],[3,1],[1,0],[4,7],[7,3],[7,3],[6,4],[2,1],[5,0],[3,1],[2,7],[6,5],[3,6],[6,7],[1,5],[7,3],[7,0],[1,6],[6,2],[1,3],[2,1],[2,1],[5,7],[0,5],[4,0],[6,4],[3,6],[6,1],[5,1],[1,0],[5,0],[7,5],[2,7],[4,5],[0,5],[1,0],[0,4],[7,1],[3,7],[7,0],[5,0],[1,3],[6,4],[6,3],[3,4],[2,3],[6,1],[1,4],[6,4],[3,6],[1,6],[4,3],[2,5],[7,0],[3,6],[5,0],[3,2],[4,1],[7,5],[7,4],[2,1],[6,3],[1,4],[7,4],[2,1],[4,0],[4,1],[5,7],[2,1],[3,2],[1,2],[5,7],[3,7],[0,7],[6,5],[7,6],[2,7],[0,3],[6,7],[7,4],[2,0],[6,0],[3,7],[4,7],[4,2],[4,3],[6,7],[5,6],[2,7],[6,3],[5,1]],[[6,7],[4,6],[2,5],[3,6],[7,6],[1,6],[1,3],[6,7],[2,6],[4,3],[6,4],[3,1],[0,1],[3,4],[0,3],[4,6],[3,0],[1,0],[6,4],[0,3],[4,0],[0,7],[5,0],[0,5],[7,0],[6,5],[1,0],[4,2],[7,3],[0,1],[6,3],[0,6],[5,4],[1,4],[5,3],[6,3],[5,7],[2,5],[0,2],[7,4],[1,4],[3,7],[5,0],[7,6],[0,3],[7,1],[2,1],[7,1],[3,5],[0,2],[4,2],[2,3],[6,5],[0,4],[1,3],[1,4],[0,7],[7,1],[4,3],[7,0],[4,7],[4,5],[3,5],[7,1],[0,4],[6,2],[3,5],[7,5],[1,4],[0,1],[4,1],[0,7],[3,4],[3,7],[7,5],[3,7],[0,7],[0,7],[4,5],[1,6],[2,6],[0,6],[6,0],[7,5],[0,4],[4,3],[7,4],[2,6],[0,4],[4,2],[5,1],[5,2],[4,6],[0,4],[6,7],[7,2],[2,7],[3,1],[1,3],[1,5],[2,1],[4,6],[7,2],[3,6],[0,3],[2,1],[0,5],[5,2],[4,1],[3,6],[6,5],[5,3],[3,2],[3,4],[2,5],[0,3],[4,7],[4,2],[3,6],[1,0],[5,0],[7,0],[4,1],[7,4],[6,5],[5,0],[0,5],[6,4],[1,4],[2,7],[2,0],[3,1],[3,2],[4,0],[1,2],[1,4],[7,0],[2,1],[0,3],[2,4],[1,4],[3,7],[5,2],[4,1],[6,7],[5,1],[2,1],[2,7],[5,2],[1,6],[7,4],[1,3],[3,2],[7,0],[7,1],[4,7],[6,3],[6,0],[4,0],[1,6],[0,7],[2,7],[3,7],[7,1],[7,4],[5,2],[0,3],[0,6],[4,6],[0,1],[2,1],[2,3],[5,0],[5,3],[5,7],[1,3],[4,5],[1,6],[6,3],[5,3],[0,2],[1,7],[6,7],[4,7],[0,3],[0,3],[1,6],[2,4],[5,3],[6,4],[1,4],[7,3],[0,4],[3,4],[4,0],[5,3],[4,0],[5,2],[6,2],[3,6],[3,1],[7,3],[5,4],[0,3],[5,4],[5,1],[6,5],[6,5],[6,7],[1,4],[6,4],[2,7],[2,6],[2,5],[7,5],[7,1],[4,1],[7,1],[3,7],[0,5],[5,1],[1,3],[4,1],[0,6],[0,7],[4,0],[0,2],[1,5],[1,0],[0,5],[2,6],[5,0],[4,0],[5,7],[4,3],[1,5],[0,7],[2,3],[5,6],[3,0],[6,5],[3,1],[3,7],[0,3],[5,0],[5,1],[0,3],[6,0],[3,2],[7,3],[0,1],[5,6],[3,7],[2,3],[0,5],[6,4],[6,1],[4,6],[0,7],[7,3],[1,6],[1,6],[0,6],[4,5],[2,7],[4,1],[0,7],[0,7],[4,7],[3,0],[6,7],[0,1],[3,7],[0,1],[2,7],[4,1],[7,4],[2,1],[7,5],[3,5],[1,6],[7,1],[6,0],[2,1],[2,3],[5,7],[7,0],[5,7],[1,0],[3,4],[3,4],[3,5],[0,7],[6,5],[5,2],[1,4],[2,1],[5,7],[5,4],[7,2],[7,0],[6,5],[3,2],[2,6],[3,1],[5,7],[3,7],[4,6],[4,7],[1,2],[0,5],[7,3],[3,1],[3,2],[2,6],[5,2],[2,5],[5,7],[5,0],[6,4],[4,2],[6,0],[4,7],[0,4],[4,1],[1,6],[5,1],[2,0],[4,1],[4,7],[4,1],[4,1],[2,4],[7,1],[1,3],[6,3],[1,2],[3,1],[2,7],[1,6],[7,2],[7,3],[4,7],[6,2],[7,5],[6,4],[7,5],[2,3],[0,7],[2,0],[5,3],[5,0],[5,7],[5,7],[3,2],[6,2],[4,3],[6,2],[3,0],[7,4],[5,4],[1,2],[5,0],[3,4],[6,7],[5,2],[1,3],[0,3],[3,2],[6,0],[2,3],[5,7],[0,2],[5,3],[1,6],[0,5],[2,0],[1,7],[3,5],[5,0],[4,6],[7,6],[2,4],[6,0],[3,5],[4,6],[6,7],[2,4],[4,6],[3,2],[5,4],[5,2],[7,6],[6,2],[6,7],[4,1],[7,1],[3,5],[2,1],[4,1],[7,0],[3,5],[2,5],[3,0],[7,2],[3,4],[1,2],[3,7],[6,0],[1,2],[1,4],[1,7],[0,4],[6,3],[4,6],[7,5],[5,7],[7,2],[7,5],[2,1],[5,4],[1,3],[3,7],[4,6],[7,0],[4,2],[4,2],[3,5],[4,6],[3,1],[5,3],[2,1],[4,1],[6,4],[6,1],[3,7],[0,3],[4,6],[4,3],[0,7],[3,6],[7,6],[4,1],[3,4],[3,1],[0,6],[5,1],[6,3],[2,7],[6,5],[7,1],[4,5],[5,6],[4,1],[3,2],[1,6],[7,5],[0,6],[7,1],[4,0],[6,0],[2,4],[5,6],[5,3],[3,5],[1,0],[2,1],[0,1],[5,7],[3,2],[1,5],[7,3],[7,5],[3,0],[4,0],[0,2],[2,7],[7,5],[6,2],[2,3],[2,1],[2,6],[3,4],[3,7],[3,7],[5,0],[0,7],[3,7],[5,6],[2,0],[7,4],[5,3],[2,6],[0,4],[6,2],[4,1],[1,5],[7,4],[1,6],[1,0],[2,1],[2,6],[1,7],[2,3],[0,3],[3,6],[1,7],[4,3],[6,4],[2,3],[4,3],[2,0]],[[0,3],[7,5],[1,4],[4,7],[7,5],[0,6],[2,0],[2,5],[7,1],[5,3],[0,1],[2,3],[0,3],[5,4],[5,3],[2,1],[7,4],[6,3],[3,0],[0,6],[5,7],[0,1],[6,5],[7,6],[2,0],[2,1],[4,2],[0,4],[5,4],[4,6],[0,4],[0,4],[1,0],[5,7],[7,2],[5,0],[5,0],[6,7],[1,4],[0,4],[7,4],[1,6],[6,7],[7,6],[0,1],[3,1],[0,7],[1,3],[7,5],[3,1],[3,0],[1,0],[6,5],[4,7],[4,6],[5,3],[2,5],[4,0],[3,2],[4,3],[3,4],[7,4],[1,7],[1,3],[0,3],[6,3],[6,4],[4,3],[6,4],[3,4],[0,4],[2,5],[6,7],[5,4],[2,6],[5,6],[0,6],[0,5],[3,5],[1,7],[2,0],[5,7],[3,2],[5,0],[1,7],[5,1],[6,5],[4,3],[2,7],[3,0],[5,0],[0,4],[7,0],[0,1],[6,0],[0,7],[4,0],[1,0],[7,1],[4,2],[7,4],[0,6],[3,6],[1,4],[5,1],[3,5],[6,1],[1,3],[5,2],[0,6],[5,0],[0,2],[0,3],[3,2],[1,2],[2,4],[5,1],[6,0],[6,5],[7,1],[4,6],[6,3],[6,7],[3,1],[1,2],[5,2],[4,7],[4,6],[7,1],[4,2],[6,0],[2,5],[3,2],[0,5],[4,0],[7,5],[0,5],[6,4],[3,6],[3,4],[6,1],[3,6],[1,7],[1,7],[4,7],[1,3],[3,2],[4,7],[7,3],[2,0],[6,7],[2,5],[4,6],[6,7],[4,0],[4,0],[6,4],[1,7],[4,1],[3,1],[5,4],[3,6],[3,7],[6,1],[2,0],[6,5],[7,2],[7,2],[2,6],[1,3],[6,7],[5,7],[2,0],[1,6],[1,6],[6,4],[4,6],[4,7],[6,7],[0,4],[7,4],[0,3],[0,4],[3,0],[2,0],[7,4],[7,6],[2,3],[1,0],[0,2],[6,5],[7,5],[6,7],[3,6],[1,7],[2,0],[3,1],[1,2],[3,6],[7,1],[4,2],[3,5],[3,4],[4,3],[6,1],[0,7],[1,3],[4,2],[1,5],[3,6],[3,4],[1,5],[1,6],[6,1],[2,3],[0,5],[3,1],[6,0],[7,2],[4,5],[0,7],[0,5],[1,0],[1,3],[7,4],[4,3],[5,0],[2,0],[5,2],[6,4],[4,1],[2,3],[2,7],[0,7],[1,7],[3,2],[4,2],[7,6],[6,1],[1,2],[4,0],[3,7],[6,1],[1,7],[3,7],[4,6],[1,7],[3,2],[0,3],[2,5],[2,3],[6,0],[7,4],[0,7],[3,2],[4,6],[1,6],[1,0],[2,0],[2,3],[6,7],[1,4],[4,7],[2,7],[6,3],[5,2],[4,6],[6,1],[0,3],[4,2],[6,3],[0,2],[7,6],[4,0],[1,2],[7,6],[3,6],[3,0],[6,0],[1,4],[2,5],[2,7],[2,0],[5,0],[1,3],[5,7],[5,0],[0,1],[0,6],[6,7],[6,7],[4,7],[7,4],[5,3],[3,5],[4,0],[3,1],[7,1],[7,6],[4,2],[7,5],[0,7],[6,0],[2,7],[5,3],[3,7],[5,4],[7,3],[1,0],[5,3],[2,3],[3,2],[5,0],[6,1],[4,5],[1,0],[1,7],[4,5],[5,7],[1,0],[1,4],[3,2],[7,4],[6,7],[7,5],[7,4],[3,6],[7,6],[5,4],[5,3],[1,4],[7,3],[5,1],[4,6],[6,3],[7,0],[0,3],[0,6],[0,5],[4,7],[1,0],[6,7],[4,3],[1,5],[1,7],[4,3],[2,5],[1,7],[7,6],[7,5],[5,7],[7,2],[6,5],[4,0],[1,0],[7,4],[6,2],[4,2],[4,3],[6,2],[5,3],[4,7],[3,4],[7,3],[2,6],[6,0],[4,5],[3,1],[7,2],[2,7],[7,1],[3,0],[0,4],[0,7],[5,2],[0,5],[5,2],[5,2],[7,6],[1,7],[5,2],[2,4],[6,5],[6,2],[0,7],[5,3],[1,4],[6,3],[0,6],[4,0],[0,4],[6,7],[1,3],[7,2],[5,2],[2,3],[4,7],[5,0],[4,2],[4,6],[7,4],[3,0],[0,4],[5,6],[0,5],[7,0],[6,2],[7,5],[0,6],[1,4],[4,6],[7,3],[1,5],[7,1],[0,6],[1,7],[3,5],[1,7],[3,6],[1,6],[7,0],[7,4],[5,1],[0,3],[2,5],[5,0],[0,6],[3,7],[1,3],[4,2],[6,1],[1,3],[1,2],[2,1],[4,2],[1,2],[6,7],[2,7],[4,1],[4,5],[3,1],[4,5],[0,5],[1,2],[3,6],[4,2],[2,4],[7,6],[4,1],[7,5],[2,7],[5,6],[6,2],[5,0],[5,4],[3,5],[5,6],[3,7],[3,7],[2,4],[0,6],[1,4],[5,6],[5,2],[2,5],[6,0],[6,1],[5,2],[0,4],[1,5],[0,5],[5,3],[7,3],[2,3],[6,3],[5,7],[6,1],[5,6],[0,7],[6,3],[3,2],[3,6],[4,1],[6,0],[3,0],[3,6],[3,2],[6,5],[7,1],[2,3],[3,1],[3,0],[0,1],[0,5],[4,2],[3,5],[3,2],[7,5],[0,4],[3,4],[3,4],[1,6],[1,0],[7,6],[3,6],[0,4],[5,2],[2,6],[5,1],[0,1],[2,3],[4,3]]]
ZW = 1092
def setup_inputs(rng):
    return {"z": rng.standard_normal((N, 128, ZW), dtype=np.float32), "g": rng.random((N, 128, T * K), dtype=np.float32)}
def reference(z, g):
    y = np.zeros((N, 128, T), np.float64)
    fill = [0] * N
    for r in range(N):
        for t in range(T):
            for k, e in enumerate(ROUTE[r][t]):
                y[r][:, t] += g[r][:, t * K + k].astype(np.float64) * z[e][:, fill[e]].astype(np.float64)
                fill[e] += 1
    return {"y": y.astype(z.dtype)}

@@ -1,0 +1,242 @@
+import numpy as np
+from concourse.mybir import AluOpType
+
+NR, NT, KK = 8, 512, 2
+NW, WT, WJ = 8, 64, 128
+LW = 168
+
+RELAY = {5: 4, 6: 5, 7: 6}
+SEND_ORDER = [5, 1, 6, 2, 7, 3, 4]
+ARRIVE_ORDER = [0, 1, 2, 5, 3, 6, 4, 7]
+BUILDERS = [(True, 0, 100), (True, 1, 100), (True, 2, 100), (True, 7, 100),
+            (True, 4, 92), (True, 5, 92), (True, 6, 92),
+            (False, 2, 88), (False, 3, 88), (False, 6, 88), (False, 7, 84)]
+
+SCRATCH = {
+    "zs": ("sbuf", [128, 1092], "float32"),
+    "gs": ("sbuf", [128, 1024], "float32"),
+    "land": ("sbuf", [128, NR * LW], "float32"),
+    "mix": ("sbuf", [128, 1024], "float32"),
+    "zt": ("sbuf", [128, 1024], "float32"),
+    "S": ("sbuf", [128, 1024], "float32"),
+    "H": ("sbuf", [128, 1024], "float32"),
+    "prod": ("sbuf", [128, 1024], "float32"),
+    "ysb": ("sbuf", [128, 512], "float32"),
+    "ida": ("sbuf", [128, 129], "float32"),
+    "ident": ("sbuf", [128, 128], "float32"),
+    "d_id": ("dram", [129, 128], "float32"),
+    "p1": ("psum", [128, 2048], "float32"),
+    "p2": ("psum", [128, 2048], "float32"),
+}
+SEMAPHORES = ["zla", "zlb", "gl", "idm", "id1", "id2", "sent", "rel", "sS", "bz", "built",
+              "mixed", "t1d", "evd", "t2d", "mud", "addd", "stored"] + ["arr%d" % e for e in range(NR)]
+
+_CACHE = {}
+
+
+def plan(route):
+    if "p" in _CACHE:
+        return _CACHE["p"]
+    slots = [[[] for _ in range(NR)] for _ in range(NR)]
+    for r in range(NR):
+        for t in range(NT):
+            for k in range(KK):
+                slots[r][route[r][t][k]].append(t * KK + k)
+    cnt = [[len(slots[r][e]) for r in range(NR)] for e in range(NR)]
+    off = [[sum(cnt[e][:r]) for r in range(NR)] for e in range(NR)]
+    pieces = [[[] for _ in range(NR)] for _ in range(NR)]
+    src = [[0] * (NT * KK) for _ in range(NR)]
+    for r in range(NR):
+        fill = [0] * NW
+        for e in range(NR):
+            js = slots[r][e]
+            for w in range(NW):
+                idx = [i for i, j in enumerate(js) if j // WJ == w]
+                if not idx:
+                    continue
+                pieces[r][e].append((w, idx[0], len(idx), fill[w]))
+                for i in idx:
+                    src[r][js[i]] = fill[w] + i - idx[0]
+                fill[w] += len(idx)
+    _CACHE["p"] = (cnt, off, pieces, src)
+    return _CACHE["p"]
+
+
+def chunks():
+    out, a = [], 0
+    for (own, k, n) in BUILDERS:
+        out.append((own, k, a, a + n))
+        a += n
+    return out
+
+
+def build_S(g, T, topo, core, rcore, src_r, a, b):
+    v, pe, sy, sem = g.vector, g.tensor, g.sync, T.sem
+    n = b - a
+    v.memset(T.ida[:, 1:128], 0.0).then_inc(sem.idm, 1)
+    v.memset(T.ida[:, 0:1], 1.0).then_inc(sem.idm, 1)
+    v.memset(T.ida[:, 128:129], -1.0).then_inc(sem.idm, 1)
+    sy.wait_ge(sem.idm, 3)
+    sy.dma_start(T.d_id[:], T.ida[:]).then_inc(sem.id1, 16)
+    sy.wait_ge(sem.id1, 16)
+    sy.dma_start(T.ident[:], T.d_id[0:128, :]).then_inc(sem.id2, 16)
+    v.memset(T.H[:, a:b], 0.0).then_inc(sem.bz, 1)
+    v.wait_ge(sem.bz, 1)
+    for j in range(a, b):
+        v.memset(T.H[0:src_r[j] + 1, j:j + 1], 1.0).then_inc(sem.built, 1)
+    pe.wait_ge(sem.id2, 16)
+    pe.wait_ge(sem.built, n)
+    pe.matmul(T.p1[:, 0:n], T.ident[:], T.H[:, a:b], True, True).then_inc(sem.t1d, 1)
+    v.wait_ge(sem.t1d, 1)
+    v.tensor_copy(T.S[:, a:b], T.p1[:, 0:n]).then_inc(sem.evd, 1)
+    g.wait_ge(sem.evd, 1)
+    rid, pid, _s = topo.addr(rcore)
+    m = topo.mask(core, rcore)
+    g.remote_dma(T.S[:, a:b], T.S[:, a:b], sem.sS, sem.sent, pid, rid, m)
+    return 16 if m == 0xFFFF else 8
+
+
+def helper_program(g, core, T, topo):
+    cnt, off, pieces, src = plan(T.tables["ROUTE"])
+    ch, k = core // 8, core % 8
+    own = (ch % 2 == 1)
+    rcore = (ch | 1) * 8 + 3
+    r = T.rank_of(rcore)
+    if r is None:
+        return
+    sent = 0
+    if own:
+        for d, hk in RELAY.items():
+            if hk == k:
+                dst = (r + d) % NR
+                n = cnt[r][dst]
+                rid, pid, _s = topo.addr(T.cores[dst])
+                g.wait_ge(T.sem.rel, 8)
+                g.remote_dma(T.land[:, r * LW:r * LW + n], T.land[:, 0:n], T.sem["arr%d" % r], T.sem.sent,
+                             pid, rid, 0x00FF)
+                sent += 8
+    for (o, hk, a, b) in chunks():
+        if o == own and hk == k:
+            sent += build_S(g, T, topo, core, rcore, src[r], a, b)
+    if sent:
+        g.wait_ge(T.sem.sent, sent)
+
+
+def rank_program(g, core, T, topo):
+    r = T.rank_of(core)
+    if r is None:
+        helper_program(g, core, T, topo)
+        return
+    cnt, off, pieces, src = plan(T.tables["ROUTE"])
+    sem = T.sem
+    v, pe, sy, sc = g.vector, g.tensor, g.sync, g.scalar
+    tot = off[r][NR - 1] + cnt[r][NR - 1]
+    half = off[r][4]
+
+    sy.dma_start(T.zs[:, 0:half], T.z[:, 0:half]).then_inc(sem.zla, 16)
+    sc.dma_start(T.zs[:, half:tot], T.z[:, half:tot]).then_inc(sem.zlb, 16)
+    sy.dma_start(T.gs[:, 0:512], T.g[:, 0:512]).then_inc(sem.gl, 16)
+    sc.dma_start(T.gs[:, 512:1024], T.g[:, 512:1024]).then_inc(sem.gl, 16)
+
+    v.memset(T.ida[:, 1:129], 0.0).then_inc(sem.idm, 1)
+    v.memset(T.ida[:, 0:1], 1.0).then_inc(sem.idm, 1)
+    sc.wait_ge(sem.idm, 2)
+    sc.dma_start(T.d_id[:], T.ida[:]).then_inc(sem.id1, 16)
+    sc.wait_ge(sem.id1, 16)
+    sc.dma_start(T.ident[:], T.d_id[0:128, :]).then_inc(sem.id2, 16)
+
+    waited = set()
+    for d in SEND_ORDER:
+        dst = (r + d) % NR
+        zl = "zla" if dst < 4 else "zlb"
+        if zl not in waited:
+            g.wait_ge(sem[zl], 16)
+            waited.add(zl)
+        n, o = cnt[r][dst], off[r][dst]
+        if d in RELAY:
+            hc = (core // 8) * 8 + RELAY[d]
+            rid, pid, _s = topo.addr(hc)
+            g.remote_dma(T.land[:, 0:n], T.zs[:, o:o + n], sem.rel, sem.sent, pid, rid, 0xFF00)
+        else:
+            rid, pid, _s = topo.addr(T.cores[dst])
+            g.remote_dma(T.land[:, r * LW:r * LW + n], T.zs[:, o:o + n], sem["arr%d" % r], sem.sent,
+                         pid, rid, 0x00FF)
+    for zl in ("zla", "zlb"):
+        if zl not in waited:
+            g.wait_ge(sem[zl], 16)
+    g.wait_ge(sem.sent, 8 * len(SEND_ORDER))
+
+    nmix = 0
+    need = [0] * NW
+    for d in ARRIVE_ORDER:
+        e = (r - d) % NR
+        if d == 0:
+            v.wait_ge(sem["zla" if r < 4 else "zlb"], 16)
+            buf, base = T.zs, off[r][r]
+        else:
+            v.wait_ge(sem["arr%d" % e], 8)
+            buf, base = T.land, e * LW
+        for (w, cs, n, po) in pieces[r][e]:
+            v.tensor_copy(T.mix[:, w * WJ + po:w * WJ + po + n], buf[:, base + cs:base + cs + n]).then_inc(sem.mixed, 1)
+            nmix += 1
+            need[w] = nmix
+
+    def bank(buf, w):
+        return buf[:, (w % 4) * 512:(w % 4) * 512 + WJ]
+
+    def win(buf, w):
+        return buf[:, w * WJ:(w + 1) * WJ]
+
+    s_total = sum(16 if own else 8 for (own, _k, _n) in BUILDERS)
+
+    def t1(w):
+        pe.wait_ge(sem.mixed, need[w])
+        if w >= 4:
+            pe.wait_ge(sem.evd, w - 3)
+        pe.matmul(bank(T.p1, w), win(T.mix, w), T.ident[:], True, True).then_inc(sem.t1d, 1)
+
+    def t2(w):
+        pe.wait_ge(sem.evd, w + 1)
+        if w == 0:
+            pe.wait_ge(sem.sS, s_total)
+        if w >= 4:
+            pe.wait_ge(sem.mud, w - 3)
+        pe.matmul(bank(T.p2, w), win(T.zt, w), win(T.S, w), True, True).then_inc(sem.t2d, 1)
+
+    pe.wait_ge(sem.id2, 16)
+    for w in range(4):
+        t1(w)
+    for w in range(4):
+        t2(w)
+        t1(w + 4)
+    for w in range(4, 8):
+        t2(w)
+
+    def evac(w):
+        v.wait_ge(sem.t1d, w + 1)
+        v.tensor_copy(win(T.zt, w), bank(T.p1, w)).then_inc(sem.evd, 1)
+
+    def mult(w):
+        v.wait_ge(sem.t2d, w + 1)
+        v.tensor_tensor(win(T.prod, w), bank(T.p2, w), win(T.gs, w), AluOpType.mult).then_inc(sem.mud, 1)
+
+    def add(w):
+        v.wait_ge(sem.mud, w + 1)
+        v.tensor_tensor(T.ysb[:, w * WT:(w + 1) * WT], T.prod[:, w * WJ:(w + 1) * WJ:2],
+                        T.prod[:, w * WJ + 1:(w + 1) * WJ:2], AluOpType.add).then_inc(sem.addd, 1)
+
+    for w in range(4):
+        evac(w)
+    v.wait_ge(sem.gl, 32)
+    for w in range(4):
+        mult(w)
+        evac(w + 4)
+        add(w)
+    for w in range(4, 8):
+        mult(w)
+        add(w)
+
+    for i, q in enumerate((sy, sc, sy, sc)):
+        q.wait_ge(sem.addd, 2 * i + 2)
+        q.dma_start(T.y[:, i * 128:(i + 1) * 128], T.ysb[:, i * 128:(i + 1) * 128]).then_inc(sem.stored, 16)
+    sy.wait_ge(sem.stored, 64)

@@ -1,4 +1,5 @@
 import numpy as np
+from concourse.bass import DstId, RemoteDMATransfer
 from concourse.mybir import AluOpType
 
 NR, NT, KK = 8, 512, 2
@@ -8,9 +9,13 @@ LW = 168
 RELAY = {5: 4, 6: 5, 7: 6}
 SEND_ORDER = [5, 1, 6, 2, 7, 3, 4]
 ARRIVE_ORDER = [0, 1, 2, 5, 3, 6, 4, 7]
-BUILDERS = [(True, 0, 100), (True, 1, 100), (True, 2, 100), (True, 7, 100),
-            (True, 4, 92), (True, 5, 92), (True, 6, 92),
-            (False, 2, 88), (False, 3, 88), (False, 6, 88), (False, 7, 84)]
+OWNER = {0: 0, 1: 1, 2: 2, 3: 7}
+OWNER_MASK = {0: 0x000F, 1: 0x00F0, 2: 0x0F00, 3: 0xF000}
+RANKW = [4, 5, 6, 7]
+NST = 2
+BUILDERS = [(True, 0, 48), (True, 1, 48), (True, 2, 48), (True, 7, 48),
+            (True, 4, 44), (True, 5, 44), (True, 6, 44),
+            (False, 2, 48), (False, 3, 48), (False, 6, 48), (False, 7, 44)]
 
 SCRATCH = {
     "zs": ("sbuf", [128, 1092], "float32"),
@@ -23,13 +28,17 @@ SCRATCH = {
     "prod": ("sbuf", [128, 1024], "float32"),
     "ysb": ("sbuf", [128, 512], "float32"),
     "ida": ("sbuf", [128, 129], "float32"),
-    "ident": ("sbuf", [128, 128], "float32"),
-    "d_id": ("dram", [129, 128], "float32"),
+    "idb": ("sbuf", [128, 129], "float32"),
+    "dmat": ("sbuf", [128, 128], "float32"),
+    "eye": ("sbuf", [128, 128], "float32"),
+    "d_ia": ("dram", [129, 128], "float32"),
+    "d_ib": ("dram", [129, 128], "float32"),
     "p1": ("psum", [128, 2048], "float32"),
     "p2": ("psum", [128, 2048], "float32"),
 }
-SEMAPHORES = ["zla", "zlb", "gl", "idm", "id1", "id2", "sent", "rel", "sS", "bz", "built",
-              "mixed", "t1d", "evd", "t2d", "mud", "addd", "stored"] + ["arr%d" % e for e in range(NR)]
+SEMAPHORES = (["zla", "zlb", "gla", "glb", "idm", "id1", "id2", "iem", "ie1", "ie2", "sent", "rel", "bz", "built",
+               "mixed", "t1d", "evd", "t2d", "mud", "addd", "stored", "sS", "gfw", "fw", "yarr",
+               "o1", "o2", "o3", "o4", "o5"] + ["arr%d" % e for e in range(NR)])
 
 _CACHE = {}
 
@@ -62,42 +71,93 @@ def plan(route):
     return _CACHE["p"]
 
 
-def chunks():
-    out, a = [], 0
-    for (own, k, n) in BUILDERS:
-        out.append((own, k, a, a + n))
-        a += n
+def chunks(own, k):
+    out = []
+    for st in range(NST):
+        a = st * (1024 // NST)
+        for (o, hk, n) in BUILDERS:
+            if o == own and hk == k:
+                out.append((a, a + n))
+            a += n
     return out
 
 
-def build_S(g, T, topo, core, rcore, src_r, a, b):
-    v, pe, sy, sem = g.vector, g.tensor, g.sync, T.sem
-    n = b - a
-    v.memset(T.ida[:, 1:128], 0.0).then_inc(sem.idm, 1)
-    v.memset(T.ida[:, 0:1], 1.0).then_inc(sem.idm, 1)
-    v.memset(T.ida[:, 128:129], -1.0).then_inc(sem.idm, 1)
-    sy.wait_ge(sem.idm, 3)
-    sy.dma_start(T.d_id[:], T.ida[:]).then_inc(sem.id1, 16)
-    sy.wait_ge(sem.id1, 16)
-    sy.dma_start(T.ident[:], T.d_id[0:128, :]).then_inc(sem.id2, 16)
-    v.memset(T.H[:, a:b], 0.0).then_inc(sem.bz, 1)
-    v.wait_ge(sem.bz, 1)
-    for j in range(a, b):
-        v.memset(T.H[0:src_r[j] + 1, j:j + 1], 1.0).then_inc(sem.built, 1)
+def parts(a, b):
+    out, x = [], a
+    while x < b:
+        e = min(b, (x // WJ + 1) * WJ)
+        k = OWNER.get(x // WJ, 3)
+        if out and out[-1][2] == k:
+            out[-1] = (out[-1][0], e, k)
+        else:
+            out.append((x, e, k))
+        x = e
+    return out
+
+
+def s_incoming(k):
+    tot = 0
+    for (o, hk, _n) in BUILDERS:
+        for (a, b) in chunks(o, hk):
+            for (_a, _b, dk) in parts(a, b):
+                if dk == k and not (o and hk == k):
+                    tot += 16 if o else 8
+    return tot
+
+
+def band(T, v, q, sb, dram, out, s_m, s_1, s_2, last):
+    v.memset(sb[:, 1:128], 0.0).then_inc(s_m, 1)
+    v.memset(sb[:, 0:1], 1.0).then_inc(s_m, 1)
+    v.memset(sb[:, 128:129], last).then_inc(s_m, 1)
+    q.wait_ge(s_m, 3)
+    q.dma_start(dram[:], sb[:]).then_inc(s_1, 16)
+    q.wait_ge(s_1, 16)
+    q.dma_start(out[:], dram[0:128, :]).then_inc(s_2, 16)
+
+
+def build_S(g, T, topo, core, src_r, chs):
+    v, pe, sem = g.vector, g.tensor, T.sem
+    band(T, v, g.sync, T.ida, T.d_ia, T.dmat, sem.idm, sem.id1, sem.id2, -1.0)
+    for (a, b) in chs:
+        v.memset(T.H[:, a:b], 0.0).then_inc(sem.bz, 1)
+    v.wait_ge(sem.bz, len(chs))
     pe.wait_ge(sem.id2, 16)
-    pe.wait_ge(sem.built, n)
-    pe.matmul(T.p1[:, 0:n], T.ident[:], T.H[:, a:b], True, True).then_inc(sem.t1d, 1)
-    v.wait_ge(sem.t1d, 1)
-    v.tensor_copy(T.S[:, a:b], T.p1[:, 0:n]).then_inc(sem.evd, 1)
-    g.wait_ge(sem.evd, 1)
-    rid, pid, _s = topo.addr(rcore)
-    m = topo.mask(core, rcore)
-    g.remote_dma(T.S[:, a:b], T.S[:, a:b], sem.sS, sem.sent, pid, rid, m)
-    return 16 if m == 0xFFFF else 8
+
+    def evac(st):
+        a, b = chs[st]
+        v.wait_ge(sem.t1d, st + 1)
+        v.tensor_copy(T.S[:, a:b], T.p1[:, st * 512:st * 512 + b - a]).then_inc(sem.evd, 1)
+
+    done = 0
+    for st, (a, b) in enumerate(chs):
+        for i, j in enumerate(range(a, b)):
+            if st > 0 and i == 8:
+                evac(st - 1)
+            v.memset(T.H[0:src_r[j] + 1, j:j + 1], 1.0).then_inc(sem.built, 1)
+        done += b - a
+        pe.wait_ge(sem.built, done)
+        pe.matmul(T.p1[:, st * 512:st * 512 + b - a], T.dmat[:], T.H[:, a:b], True, True).then_inc(sem.t1d, 1)
+    evac(len(chs) - 1)
+    sent, local = 0, []
+    rchip = (core // 8) | 1
+    for st, (a, b) in enumerate(chs):
+        g.wait_ge(sem.evd, st + 1)
+        for (pa, pb, dk) in parts(a, b):
+            dc = rchip * 8 + dk
+            if dc == core:
+                local.append(st)
+                continue
+            rid, pid, _s = topo.addr(dc)
+            m = topo.mask(core, dc)
+            g.remote_dma(T.S[:, pa:pb], T.S[:, pa:pb], sem.sS, sem.sent, pid, rid, m)
+            sent += 16 if m == 0xFFFF else 8
+    return sent, local
 
 
 def helper_program(g, core, T, topo):
     cnt, off, pieces, src = plan(T.tables["ROUTE"])
+    sem = T.sem
+    v, pe = g.vector, g.tensor
     ch, k = core // 8, core % 8
     own = (ch % 2 == 1)
     rcore = (ch | 1) * 8 + 3
@@ -105,21 +165,49 @@ def helper_program(g, core, T, topo):
     if r is None:
         return
     sent = 0
+    mine = [w for w, hk in OWNER.items() if own and hk == k]
+    if mine:
+        band(T, v, g.scalar, T.idb, T.d_ib, T.eye, sem.iem, sem.ie1, sem.ie2, 0.0)
     if own:
         for d, hk in RELAY.items():
             if hk == k:
                 dst = (r + d) % NR
                 n = cnt[r][dst]
                 rid, pid, _s = topo.addr(T.cores[dst])
-                g.wait_ge(T.sem.rel, 8)
-                g.remote_dma(T.land[:, r * LW:r * LW + n], T.land[:, 0:n], T.sem["arr%d" % r], T.sem.sent,
+                g.wait_ge(sem.rel, 8)
+                g.remote_dma(T.land[:, r * LW:r * LW + n], T.land[:, 0:n], sem["arr%d" % r], sem.sent,
                              pid, rid, 0x00FF)
                 sent += 8
-    for (o, hk, a, b) in chunks():
-        if o == own and hk == k:
-            sent += build_S(g, T, topo, core, rcore, src[r], a, b)
+    chs = chunks(own, k)
+    local = []
+    if chs:
+        s, local = build_S(g, T, topo, core, src[r], chs)
+        sent += s
+    for w in mine:
+        cw = slice(w * WJ, (w + 1) * WJ)
+        pe.wait_ge(sem.ie2, 16)
+        pe.wait_ge(sem.fw, 4)
+        pe.matmul(T.p2[:, 0:WJ], T.mix[:, cw], T.eye[:], True, True).then_inc(sem.o1, 1)
+        v.wait_ge(sem.o1, 1)
+        v.tensor_copy(T.zt[:, cw], T.p2[:, 0:WJ]).then_inc(sem.o2, 1)
+        pe.wait_ge(sem.o2, 1)
+        pe.wait_ge(sem.sS, s_incoming(k))
+        if local:
+            pe.wait_ge(sem.evd, max(local) + 1)
+        pe.matmul(T.p2[:, 512:512 + WJ], T.zt[:, cw], T.S[:, cw], True, True).then_inc(sem.o3, 1)
+        v.wait_ge(sem.o3, 1)
+        v.wait_ge(sem.gfw, 4)
+        v.tensor_tensor(T.prod[:, cw], T.p2[:, 512:512 + WJ], T.gs[:, cw], AluOpType.mult).then_inc(sem.o4, 1)
+        v.wait_ge(sem.o4, 1)
+        v.tensor_tensor(T.ysb[:, w * WT:(w + 1) * WT], T.prod[:, w * WJ:(w + 1) * WJ:2],
+                        T.prod[:, w * WJ + 1:(w + 1) * WJ:2], AluOpType.add).then_inc(sem.o5, 1)
+        g.wait_ge(sem.o5, 1)
+        rid, pid, _s = topo.addr(rcore)
+        g.remote_dma(T.ysb[:, w * WT:(w + 1) * WT], T.ysb[:, w * WT:(w + 1) * WT], sem.yarr, sem.sent,
+                     pid, rid, 0xFFFF)
+        sent += 16
     if sent:
-        g.wait_ge(T.sem.sent, sent)
+        g.wait_ge(sem.sent, sent)
 
 
 def rank_program(g, core, T, topo):
@@ -132,20 +220,16 @@ def rank_program(g, core, T, topo):
     v, pe, sy, sc = g.vector, g.tensor, g.sync, g.scalar
     tot = off[r][NR - 1] + cnt[r][NR - 1]
     half = off[r][4]
+    nf = len(OWNER)
 
     sy.dma_start(T.zs[:, 0:half], T.z[:, 0:half]).then_inc(sem.zla, 16)
     sc.dma_start(T.zs[:, half:tot], T.z[:, half:tot]).then_inc(sem.zlb, 16)
-    sy.dma_start(T.gs[:, 0:512], T.g[:, 0:512]).then_inc(sem.gl, 16)
-    sc.dma_start(T.gs[:, 512:1024], T.g[:, 512:1024]).then_inc(sem.gl, 16)
-
-    v.memset(T.ida[:, 1:129], 0.0).then_inc(sem.idm, 1)
-    v.memset(T.ida[:, 0:1], 1.0).then_inc(sem.idm, 1)
-    sc.wait_ge(sem.idm, 2)
-    sc.dma_start(T.d_id[:], T.ida[:]).then_inc(sem.id1, 16)
-    sc.wait_ge(sem.id1, 16)
-    sc.dma_start(T.ident[:], T.d_id[0:128, :]).then_inc(sem.id2, 16)
+    sy.dma_start(T.gs[:, 0:nf * WJ], T.g[:, 0:nf * WJ]).then_inc(sem.gla, 16)
+    sc.dma_start(T.gs[:, nf * WJ:1024], T.g[:, nf * WJ:1024]).then_inc(sem.glb, 16)
+    band(T, v, sc, T.idb, T.d_ib, T.eye, sem.iem, sem.ie1, sem.ie2, 0.0)
 
     waited = set()
+    sent = 0
     for d in SEND_ORDER:
         dst = (r + d) % NR
         zl = "zla" if dst < 4 else "zlb"
@@ -161,10 +245,10 @@ def rank_program(g, core, T, topo):
             rid, pid, _s = topo.addr(T.cores[dst])
             g.remote_dma(T.land[:, r * LW:r * LW + n], T.zs[:, o:o + n], sem["arr%d" % r], sem.sent,
                          pid, rid, 0x00FF)
+        sent += 8
     for zl in ("zla", "zlb"):
         if zl not in waited:
             g.wait_ge(sem[zl], 16)
-    g.wait_ge(sem.sent, 8 * len(SEND_ORDER))
 
     nmix = 0
     need = [0] * NW
@@ -181,62 +265,62 @@ def rank_program(g, core, T, topo):
             nmix += 1
             need[w] = nmix
 
-    def bank(buf, w):
-        return buf[:, (w % 4) * 512:(w % 4) * 512 + WJ]
-
     def win(buf, w):
         return buf[:, w * WJ:(w + 1) * WJ]
 
-    s_total = sum(16 if own else 8 for (own, _k, _n) in BUILDERS)
+    def forward(buf, rsem):
+        trs = []
+        for w, hk in OWNER.items():
+            rid, pid, _s = topo.addr((core // 8) * 8 + hk)
+            trs.append(RemoteDMATransfer(dst_ids=[DstId(rid=rid, pnc=pid)], dma_engine_mask=OWNER_MASK[w],
+                                         remote_sem=rsem, src=win(buf, w), dst=win(buf, w)))
+        g.remote_dma_fused(trs, local_sem=sem.sent)
 
-    def t1(w):
-        pe.wait_ge(sem.mixed, need[w])
-        if w >= 4:
-            pe.wait_ge(sem.evd, w - 3)
-        pe.matmul(bank(T.p1, w), win(T.mix, w), T.ident[:], True, True).then_inc(sem.t1d, 1)
+    g.wait_ge(sem.gla, 16)
+    forward(T.gs, sem.gfw)
+    g.wait_ge(sem.mixed, max(need[w] for w in OWNER))
+    forward(T.mix, sem.fw)
+    sent += 32
+    g.wait_ge(sem.sent, sent)
 
-    def t2(w):
-        pe.wait_ge(sem.evd, w + 1)
-        if w == 0:
-            pe.wait_ge(sem.sS, s_total)
-        if w >= 4:
-            pe.wait_ge(sem.mud, w - 3)
-        pe.matmul(bank(T.p2, w), win(T.zt, w), win(T.S, w), True, True).then_inc(sem.t2d, 1)
+    def bank(buf, i):
+        return buf[:, i * 512:i * 512 + WJ]
 
-    pe.wait_ge(sem.id2, 16)
-    for w in range(4):
-        t1(w)
-    for w in range(4):
-        t2(w)
-        t1(w + 4)
-    for w in range(4, 8):
-        t2(w)
+    def t1(i):
+        pe.wait_ge(sem.mixed, need[RANKW[i]])
+        pe.matmul(bank(T.p1, i), win(T.mix, RANKW[i]), T.eye[:], True, True).then_inc(sem.t1d, 1)
 
-    def evac(w):
-        v.wait_ge(sem.t1d, w + 1)
-        v.tensor_copy(win(T.zt, w), bank(T.p1, w)).then_inc(sem.evd, 1)
+    def t2(i):
+        pe.wait_ge(sem.evd, i + 1)
+        if i == 0:
+            pe.wait_ge(sem.sS, s_incoming(3))
+        pe.matmul(bank(T.p2, i), win(T.zt, RANKW[i]), win(T.S, RANKW[i]), True, True).then_inc(sem.t2d, 1)
 
-    def mult(w):
-        v.wait_ge(sem.t2d, w + 1)
-        v.tensor_tensor(win(T.prod, w), bank(T.p2, w), win(T.gs, w), AluOpType.mult).then_inc(sem.mud, 1)
+    pe.wait_ge(sem.ie2, 16)
+    t1(0), t1(1), t2(0), t1(2), t2(1), t1(3), t2(2), t2(3)
 
-    def add(w):
-        v.wait_ge(sem.mud, w + 1)
+    def evac(i):
+        v.wait_ge(sem.t1d, i + 1)
+        v.tensor_copy(win(T.zt, RANKW[i]), bank(T.p1, i)).then_inc(sem.evd, 1)
+
+    def mult(i):
+        v.wait_ge(sem.t2d, i + 1)
+        v.tensor_tensor(win(T.prod, RANKW[i]), bank(T.p2, i), win(T.gs, RANKW[i]), AluOpType.mult).then_inc(sem.mud, 1)
+
+    def add(i):
+        w = RANKW[i]
+        v.wait_ge(sem.mud, i + 1)
         v.tensor_tensor(T.ysb[:, w * WT:(w + 1) * WT], T.prod[:, w * WJ:(w + 1) * WJ:2],
                         T.prod[:, w * WJ + 1:(w + 1) * WJ:2], AluOpType.add).then_inc(sem.addd, 1)
 
-    for w in range(4):
-        evac(w)
-    v.wait_ge(sem.gl, 32)
-    for w in range(4):
-        mult(w)
-        evac(w + 4)
-        add(w)
-    for w in range(4, 8):
-        mult(w)
-        add(w)
+    evac(0), evac(1)
+    v.wait_ge(sem.glb, 16)
+    mult(0), evac(2), add(0), mult(1), evac(3), add(1), mult(2), add(2), mult(3), add(3)
 
-    for i, q in enumerate((sy, sc, sy, sc)):
-        q.wait_ge(sem.addd, 2 * i + 2)
-        q.dma_start(T.y[:, i * 128:(i + 1) * 128], T.ysb[:, i * 128:(i + 1) * 128]).then_inc(sem.stored, 16)
-    sy.wait_ge(sem.stored, 64)
+    sy.wait_ge(sem.yarr, 16 * nf)
+    sy.dma_start(T.y[:, 0:nf * WT], T.ysb[:, 0:nf * WT]).then_inc(sem.stored, 16)
+    for i in (0, 1):
+        a = (RANKW[0] + 2 * i) * WT
+        sc.wait_ge(sem.addd, 2 * i + 2)
+        sc.dma_start(T.y[:, a:a + 2 * WT], T.ysb[:, a:a + 2 * WT]).then_inc(sem.stored, 16)
+    sy.wait_ge(sem.stored, 48)

@@ -1,5 +1,4 @@
 import numpy as np
-from concourse.bass import DstId, RemoteDMATransfer
 from concourse.mybir import AluOpType
 
 NR, NT, KK = 8, 512, 2
@@ -7,15 +6,14 @@ NW, WT, WJ = 8, 64, 128
 LW = 168
 
 RELAY = {5: 4, 6: 5, 7: 6}
-SEND_ORDER = [5, 1, 6, 2, 7, 3, 4]
+SEND_ORDER = [5, 0, 1, 6, 2, 7, 3, 4]
 ARRIVE_ORDER = [0, 1, 2, 5, 3, 6, 4, 7]
-OWNER = {0: 0, 1: 1, 2: 2, 3: 7}
-OWNER_MASK = {0: 0x000F, 1: 0x00F0, 2: 0x0F00, 3: 0xF000}
-RANKW = [4, 5, 6, 7]
-NST = 2
-BUILDERS = [(True, 0, 48), (True, 1, 48), (True, 2, 48), (True, 7, 48),
-            (True, 4, 44), (True, 5, 44), (True, 6, 44),
-            (False, 2, 48), (False, 3, 48), (False, 6, 48), (False, 7, 44)]
+BK = 7
+BWIN, RWIN = [0, 1, 2, 3], [4, 5, 6, 7]
+NST = 4
+BUILDERS = [(True, 0, 28), (True, 1, 28), (True, 2, 28),
+            (True, 4, 24), (True, 5, 24), (True, 6, 24),
+            (False, 2, 28), (False, 3, 24), (False, 6, 24), (False, 7, 24)]
 
 SCRATCH = {
     "zs": ("sbuf", [128, 1092], "float32"),
@@ -37,8 +35,8 @@ SCRATCH = {
     "p2": ("psum", [128, 2048], "float32"),
 }
 SEMAPHORES = (["zla", "zlb", "gla", "glb", "idm", "id1", "id2", "iem", "ie1", "ie2", "sent", "rel", "bz", "built",
-               "mixed", "t1d", "evd", "t2d", "mud", "addd", "stored", "sS", "gfw", "fw", "yarr",
-               "o1", "o2", "o3", "o4", "o5"] + ["arr%d" % e for e in range(NR)])
+               "mixed", "t1d", "evd", "t2d", "mud", "addd", "stored", "gfw", "yarr0", "yarr1"]
+              + ["arr%d" % e for e in range(NR)] + ["sS%d" % s for s in range(NST)])
 
 _CACHE = {}
 
@@ -52,6 +50,7 @@ def plan(route):
             for k in range(KK):
                 slots[r][route[r][t][k]].append(t * KK + k)
     cnt = [[len(slots[r][e]) for r in range(NR)] for e in range(NR)]
+    hc = [[len([j for j in slots[r][e] if j < 4 * WJ]) for r in range(NR)] for e in range(NR)]
     off = [[sum(cnt[e][:r]) for r in range(NR)] for e in range(NR)]
     pieces = [[[] for _ in range(NR)] for _ in range(NR)]
     src = [[0] * (NT * KK) for _ in range(NR)]
@@ -67,14 +66,19 @@ def plan(route):
                 for i in idx:
                     src[r][js[i]] = fill[w] + i - idx[0]
                 fill[w] += len(idx)
-    _CACHE["p"] = (cnt, off, pieces, src)
+    _CACHE["p"] = (cnt, off, hc, pieces, src)
     return _CACHE["p"]
+
+
+def col_of(u):
+    st, x = divmod(u, 2 * WJ)
+    return (st if x < WJ else st + 4) * WJ + x % WJ
 
 
 def chunks(own, k):
     out = []
     for st in range(NST):
-        a = st * (1024 // NST)
+        a = st * 2 * WJ
         for (o, hk, n) in BUILDERS:
             if o == own and hk == k:
                 out.append((a, a + n))
@@ -82,30 +86,26 @@ def chunks(own, k):
     return out
 
 
-def parts(a, b):
-    out, x = [], a
-    while x < b:
-        e = min(b, (x // WJ + 1) * WJ)
-        k = OWNER.get(x // WJ, 3)
-        if out and out[-1][2] == k:
-            out[-1] = (out[-1][0], e, k)
-        else:
-            out.append((x, e, k))
+def parts(ua, ub):
+    out, x = [], ua
+    while x < ub:
+        e = min(ub, (x // WJ + 1) * WJ)
+        out.append((x, e, BK if col_of(x) // WJ in BWIN else 3))
         x = e
     return out
 
 
-def s_incoming(k):
+def s_incoming(k, st):
     tot = 0
     for (o, hk, _n) in BUILDERS:
-        for (a, b) in chunks(o, hk):
-            for (_a, _b, dk) in parts(a, b):
-                if dk == k and not (o and hk == k):
-                    tot += 16 if o else 8
+        ua, ub = chunks(o, hk)[st]
+        for (_a, _b, dk) in parts(ua, ub):
+            if dk == k:
+                tot += 16 if o else 8
     return tot
 
 
-def band(T, v, q, sb, dram, out, s_m, s_1, s_2, last):
+def band(v, q, sb, dram, out, s_m, s_1, s_2, last):
     v.memset(sb[:, 1:128], 0.0).then_inc(s_m, 1)
     v.memset(sb[:, 0:1], 1.0).then_inc(s_m, 1)
     v.memset(sb[:, 128:129], last).then_inc(s_m, 1)
@@ -117,7 +117,7 @@ def band(T, v, q, sb, dram, out, s_m, s_1, s_2, last):
 
 def build_S(g, T, topo, core, src_r, chs):
     v, pe, sem = g.vector, g.tensor, T.sem
-    band(T, v, g.sync, T.ida, T.d_ia, T.dmat, sem.idm, sem.id1, sem.id2, -1.0)
+    band(v, g.sync, T.ida, T.d_ia, T.dmat, sem.idm, sem.id1, sem.id2, -1.0)
     for (a, b) in chs:
         v.memset(T.H[:, a:b], 0.0).then_inc(sem.bz, 1)
     v.wait_ge(sem.bz, len(chs))
@@ -130,34 +130,88 @@ def build_S(g, T, topo, core, src_r, chs):
 
     done = 0
     for st, (a, b) in enumerate(chs):
-        for i, j in enumerate(range(a, b)):
+        for i, u in enumerate(range(a, b)):
             if st > 0 and i == 8:
                 evac(st - 1)
-            v.memset(T.H[0:src_r[j] + 1, j:j + 1], 1.0).then_inc(sem.built, 1)
+            v.memset(T.H[0:src_r[col_of(u)] + 1, u:u + 1], 1.0).then_inc(sem.built, 1)
         done += b - a
         pe.wait_ge(sem.built, done)
         pe.matmul(T.p1[:, st * 512:st * 512 + b - a], T.dmat[:], T.H[:, a:b], True, True).then_inc(sem.t1d, 1)
     evac(len(chs) - 1)
-    sent, local = 0, []
+    sent = 0
     rchip = (core // 8) | 1
     for st, (a, b) in enumerate(chs):
         g.wait_ge(sem.evd, st + 1)
         for (pa, pb, dk) in parts(a, b):
             dc = rchip * 8 + dk
-            if dc == core:
-                local.append(st)
-                continue
             rid, pid, _s = topo.addr(dc)
             m = topo.mask(core, dc)
-            g.remote_dma(T.S[:, pa:pb], T.S[:, pa:pb], sem.sS, sem.sent, pid, rid, m)
+            ja = col_of(pa)
+            g.remote_dma(T.S[:, ja:ja + pb - pa], T.S[:, pa:pb], sem["sS%d" % st], sem.sent, pid, rid, m)
             sent += 16 if m == 0xFFFF else 8
-    return sent, local
+    return sent
+
+
+def worker(g, T, r, wins, k, own_buf, own_base, own_sem, own_val, g_sem, g_val, pieces):
+    sem = T.sem
+    v, pe = g.vector, g.tensor
+    nmix = 0
+    need = {}
+    for d in ARRIVE_ORDER:
+        e = (r - d) % NR
+        if d == 0:
+            v.wait_ge(own_sem, own_val)
+            buf, base = own_buf, own_base
+        else:
+            v.wait_ge(sem["arr%d" % e], 8)
+            buf, base = T.land, e * LW
+        for (w, cs, n, po) in pieces[r][e]:
+            if w in wins:
+                v.tensor_copy(T.mix[:, w * WJ + po:w * WJ + po + n],
+                              buf[:, base + cs:base + cs + n]).then_inc(sem.mixed, 1)
+                nmix += 1
+                need[w] = nmix
+
+    def win(buf, w):
+        return buf[:, w * WJ:(w + 1) * WJ]
+
+    def bank(buf, i):
+        return buf[:, i * 512:i * 512 + WJ]
+
+    def t1(i):
+        pe.wait_ge(sem.mixed, need[wins[i]])
+        pe.matmul(bank(T.p1, i), win(T.mix, wins[i]), T.eye[:], True, True).then_inc(sem.t1d, 1)
+
+    def t2(i):
+        pe.wait_ge(sem.evd, i + 1)
+        pe.wait_ge(sem["sS%d" % i], s_incoming(k, i))
+        pe.matmul(bank(T.p2, i), win(T.zt, wins[i]), win(T.S, wins[i]), True, True).then_inc(sem.t2d, 1)
+
+    pe.wait_ge(sem.ie2, 16)
+    t1(0), t1(1), t2(0), t1(2), t2(1), t1(3), t2(2), t2(3)
+
+    def evac(i):
+        v.wait_ge(sem.t1d, i + 1)
+        v.tensor_copy(win(T.zt, wins[i]), bank(T.p1, i)).then_inc(sem.evd, 1)
+
+    def mult(i):
+        v.wait_ge(sem.t2d, i + 1)
+        v.tensor_tensor(win(T.prod, wins[i]), bank(T.p2, i), win(T.gs, wins[i]), AluOpType.mult).then_inc(sem.mud, 1)
+
+    def add(i):
+        w = wins[i]
+        v.wait_ge(sem.mud, i + 1)
+        v.tensor_tensor(T.ysb[:, w * WT:(w + 1) * WT], T.prod[:, w * WJ:(w + 1) * WJ:2],
+                        T.prod[:, w * WJ + 1:(w + 1) * WJ:2], AluOpType.add).then_inc(sem.addd, 1)
+
+    evac(0), evac(1)
+    v.wait_ge(g_sem, g_val)
+    mult(0), evac(2), add(0), mult(1), evac(3), add(1), mult(2), add(2), mult(3), add(3)
 
 
 def helper_program(g, core, T, topo):
-    cnt, off, pieces, src = plan(T.tables["ROUTE"])
+    cnt, off, hc, pieces, src = plan(T.tables["ROUTE"])
     sem = T.sem
-    v, pe = g.vector, g.tensor
     ch, k = core // 8, core % 8
     own = (ch % 2 == 1)
     rcore = (ch | 1) * 8 + 3
@@ -165,47 +219,29 @@ def helper_program(g, core, T, topo):
     if r is None:
         return
     sent = 0
-    mine = [w for w, hk in OWNER.items() if own and hk == k]
-    if mine:
-        band(T, v, g.scalar, T.idb, T.d_ib, T.eye, sem.iem, sem.ie1, sem.ie2, 0.0)
+    if own and k == BK:
+        band(g.vector, g.scalar, T.idb, T.d_ib, T.eye, sem.iem, sem.ie1, sem.ie2, 0.0)
+        worker(g, T, r, BWIN, BK, T.land, r * LW, sem["arr%d" % r], 8, sem.gfw, 16, pieces)
+        rid, pid, _s = topo.addr(rcore)
+        for i in (0, 1):
+            g.wait_ge(sem.addd, 2 * i + 2)
+            g.remote_dma(T.ysb[:, i * WJ:(i + 1) * WJ], T.ysb[:, i * WJ:(i + 1) * WJ], sem["yarr%d" % i], sem.sent,
+                         pid, rid, 0xFFFF)
+            sent += 16
     if own:
         for d, hk in RELAY.items():
             if hk == k:
                 dst = (r + d) % NR
-                n = cnt[r][dst]
-                rid, pid, _s = topo.addr(T.cores[dst])
+                n, h = cnt[r][dst], hc[r][dst]
                 g.wait_ge(sem.rel, 8)
-                g.remote_dma(T.land[:, r * LW:r * LW + n], T.land[:, 0:n], sem["arr%d" % r], sem.sent,
-                             pid, rid, 0x00FF)
-                sent += 8
+                for (a, b, dc) in ((0, h, (T.cores[dst] // 8) * 8 + BK), (h, n, T.cores[dst])):
+                    rid, pid, _s = topo.addr(dc)
+                    g.remote_dma(T.land[:, r * LW + a:r * LW + b], T.land[:, a:b], sem["arr%d" % r], sem.sent,
+                                 pid, rid, 0x00FF)
+                    sent += 8
     chs = chunks(own, k)
-    local = []
     if chs:
-        s, local = build_S(g, T, topo, core, src[r], chs)
-        sent += s
-    for w in mine:
-        cw = slice(w * WJ, (w + 1) * WJ)
-        pe.wait_ge(sem.ie2, 16)
-        pe.wait_ge(sem.fw, 4)
-        pe.matmul(T.p2[:, 0:WJ], T.mix[:, cw], T.eye[:], True, True).then_inc(sem.o1, 1)
-        v.wait_ge(sem.o1, 1)
-        v.tensor_copy(T.zt[:, cw], T.p2[:, 0:WJ]).then_inc(sem.o2, 1)
-        pe.wait_ge(sem.o2, 1)
-        pe.wait_ge(sem.sS, s_incoming(k))
-        if local:
-            pe.wait_ge(sem.evd, max(local) + 1)
-        pe.matmul(T.p2[:, 512:512 + WJ], T.zt[:, cw], T.S[:, cw], True, True).then_inc(sem.o3, 1)
-        v.wait_ge(sem.o3, 1)
-        v.wait_ge(sem.gfw, 4)
-        v.tensor_tensor(T.prod[:, cw], T.p2[:, 512:512 + WJ], T.gs[:, cw], AluOpType.mult).then_inc(sem.o4, 1)
-        v.wait_ge(sem.o4, 1)
-        v.tensor_tensor(T.ysb[:, w * WT:(w + 1) * WT], T.prod[:, w * WJ:(w + 1) * WJ:2],
-                        T.prod[:, w * WJ + 1:(w + 1) * WJ:2], AluOpType.add).then_inc(sem.o5, 1)
-        g.wait_ge(sem.o5, 1)
-        rid, pid, _s = topo.addr(rcore)
-        g.remote_dma(T.ysb[:, w * WT:(w + 1) * WT], T.ysb[:, w * WT:(w + 1) * WT], sem.yarr, sem.sent,
-                     pid, rid, 0xFFFF)
-        sent += 16
+        sent += build_S(g, T, topo, core, src[r], chs)
     if sent:
         g.wait_ge(sem.sent, sent)
 
@@ -215,18 +251,18 @@ def rank_program(g, core, T, topo):
     if r is None:
         helper_program(g, core, T, topo)
         return
-    cnt, off, pieces, src = plan(T.tables["ROUTE"])
+    cnt, off, hc, pieces, src = plan(T.tables["ROUTE"])
     sem = T.sem
-    v, pe, sy, sc = g.vector, g.tensor, g.sync, g.scalar
+    v, sy, sc = g.vector, g.sync, g.scalar
     tot = off[r][NR - 1] + cnt[r][NR - 1]
     half = off[r][4]
-    nf = len(OWNER)
+    chip0 = (core // 8) * 8
 
     sy.dma_start(T.zs[:, 0:half], T.z[:, 0:half]).then_inc(sem.zla, 16)
     sc.dma_start(T.zs[:, half:tot], T.z[:, half:tot]).then_inc(sem.zlb, 16)
-    sy.dma_start(T.gs[:, 0:nf * WJ], T.g[:, 0:nf * WJ]).then_inc(sem.gla, 16)
-    sc.dma_start(T.gs[:, nf * WJ:1024], T.g[:, nf * WJ:1024]).then_inc(sem.glb, 16)
-    band(T, v, sc, T.idb, T.d_ib, T.eye, sem.iem, sem.ie1, sem.ie2, 0.0)
+    sy.dma_start(T.gs[:, 0:512], T.g[:, 0:512]).then_inc(sem.gla, 16)
+    sc.dma_start(T.gs[:, 512:1024], T.g[:, 512:1024]).then_inc(sem.glb, 16)
+    band(v, sc, T.idb, T.d_ib, T.eye, sem.iem, sem.ie1, sem.ie2, 0.0)
 
     waited = set()
     sent = 0
@@ -236,91 +272,32 @@ def rank_program(g, core, T, topo):
         if zl not in waited:
             g.wait_ge(sem[zl], 16)
             waited.add(zl)
-        n, o = cnt[r][dst], off[r][dst]
-        if d in RELAY:
-            hc = (core // 8) * 8 + RELAY[d]
-            rid, pid, _s = topo.addr(hc)
-            g.remote_dma(T.land[:, 0:n], T.zs[:, o:o + n], sem.rel, sem.sent, pid, rid, 0xFF00)
+        n, h, o = cnt[r][dst], hc[r][dst], off[r][dst]
+        if d == 0:
+            todo = [(0, h, r * LW, chip0 + BK, sem["arr%d" % r], 0xFF00)]
+        elif d in RELAY:
+            todo = [(0, n, 0, chip0 + RELAY[d], sem.rel, 0xFF00)]
         else:
-            rid, pid, _s = topo.addr(T.cores[dst])
-            g.remote_dma(T.land[:, r * LW:r * LW + n], T.zs[:, o:o + n], sem["arr%d" % r], sem.sent,
-                         pid, rid, 0x00FF)
-        sent += 8
+            todo = [(0, h, r * LW, (T.cores[dst] // 8) * 8 + BK, sem["arr%d" % r], 0x00FF),
+                    (h, n, r * LW, T.cores[dst], sem["arr%d" % r], 0x00FF)]
+        for (a, b, base, dc, rs, m) in todo:
+            rid, pid, _s = topo.addr(dc)
+            g.remote_dma(T.land[:, base + a:base + b], T.zs[:, o + a:o + b], rs, sem.sent, pid, rid, m)
+            sent += 8
     for zl in ("zla", "zlb"):
         if zl not in waited:
             g.wait_ge(sem[zl], 16)
-
-    nmix = 0
-    need = [0] * NW
-    for d in ARRIVE_ORDER:
-        e = (r - d) % NR
-        if d == 0:
-            v.wait_ge(sem["zla" if r < 4 else "zlb"], 16)
-            buf, base = T.zs, off[r][r]
-        else:
-            v.wait_ge(sem["arr%d" % e], 8)
-            buf, base = T.land, e * LW
-        for (w, cs, n, po) in pieces[r][e]:
-            v.tensor_copy(T.mix[:, w * WJ + po:w * WJ + po + n], buf[:, base + cs:base + cs + n]).then_inc(sem.mixed, 1)
-            nmix += 1
-            need[w] = nmix
-
-    def win(buf, w):
-        return buf[:, w * WJ:(w + 1) * WJ]
-
-    def forward(buf, rsem):
-        trs = []
-        for w, hk in OWNER.items():
-            rid, pid, _s = topo.addr((core // 8) * 8 + hk)
-            trs.append(RemoteDMATransfer(dst_ids=[DstId(rid=rid, pnc=pid)], dma_engine_mask=OWNER_MASK[w],
-                                         remote_sem=rsem, src=win(buf, w), dst=win(buf, w)))
-        g.remote_dma_fused(trs, local_sem=sem.sent)
-
     g.wait_ge(sem.gla, 16)
-    forward(T.gs, sem.gfw)
-    g.wait_ge(sem.mixed, max(need[w] for w in OWNER))
-    forward(T.mix, sem.fw)
-    sent += 32
+    rid, pid, _s = topo.addr(chip0 + BK)
+    g.remote_dma(T.gs[:, 0:512], T.gs[:, 0:512], sem.gfw, sem.sent, pid, rid, 0xFFFF)
+    sent += 16
     g.wait_ge(sem.sent, sent)
 
-    def bank(buf, i):
-        return buf[:, i * 512:i * 512 + WJ]
+    worker(g, T, r, RWIN, 3, T.zs, off[r][r], sem["zla" if r < 4 else "zlb"], 16, sem.glb, 16, pieces)
 
-    def t1(i):
-        pe.wait_ge(sem.mixed, need[RANKW[i]])
-        pe.matmul(bank(T.p1, i), win(T.mix, RANKW[i]), T.eye[:], True, True).then_inc(sem.t1d, 1)
-
-    def t2(i):
-        pe.wait_ge(sem.evd, i + 1)
-        if i == 0:
-            pe.wait_ge(sem.sS, s_incoming(3))
-        pe.matmul(bank(T.p2, i), win(T.zt, RANKW[i]), win(T.S, RANKW[i]), True, True).then_inc(sem.t2d, 1)
-
-    pe.wait_ge(sem.ie2, 16)
-    t1(0), t1(1), t2(0), t1(2), t2(1), t1(3), t2(2), t2(3)
-
-    def evac(i):
-        v.wait_ge(sem.t1d, i + 1)
-        v.tensor_copy(win(T.zt, RANKW[i]), bank(T.p1, i)).then_inc(sem.evd, 1)
-
-    def mult(i):
-        v.wait_ge(sem.t2d, i + 1)
-        v.tensor_tensor(win(T.prod, RANKW[i]), bank(T.p2, i), win(T.gs, RANKW[i]), AluOpType.mult).then_inc(sem.mud, 1)
-
-    def add(i):
-        w = RANKW[i]
-        v.wait_ge(sem.mud, i + 1)
-        v.tensor_tensor(T.ysb[:, w * WT:(w + 1) * WT], T.prod[:, w * WJ:(w + 1) * WJ:2],
-                        T.prod[:, w * WJ + 1:(w + 1) * WJ:2], AluOpType.add).then_inc(sem.addd, 1)
-
-    evac(0), evac(1)
-    v.wait_ge(sem.glb, 16)
-    mult(0), evac(2), add(0), mult(1), evac(3), add(1), mult(2), add(2), mult(3), add(3)
-
-    sy.wait_ge(sem.yarr, 16 * nf)
-    sy.dma_start(T.y[:, 0:nf * WT], T.ysb[:, 0:nf * WT]).then_inc(sem.stored, 16)
     for i in (0, 1):
-        a = (RANKW[0] + 2 * i) * WT
+        sy.wait_ge(sem["yarr%d" % i], 16)
+        sy.dma_start(T.y[:, i * WJ:(i + 1) * WJ], T.ysb[:, i * WJ:(i + 1) * WJ]).then_inc(sem.stored, 16)
         sc.wait_ge(sem.addd, 2 * i + 2)
-        sc.dma_start(T.y[:, a:a + 2 * WT], T.ysb[:, a:a + 2 * WT]).then_inc(sem.stored, 16)
-    sy.wait_ge(sem.stored, 48)
+        sc.dma_start(T.y[:, (i + 2) * WJ:(i + 3) * WJ], T.ysb[:, (i + 2) * WJ:(i + 3) * WJ]).then_inc(sem.stored, 16)
+    sy.wait_ge(sem.stored, 64)

import numpy as np
from concourse.mybir import AluOpType

NR, NT, KK = 8, 512, 2
NW, WT, WJ = 8, 64, 128
LW = 168

RELAY = {5: 4, 6: 5, 7: 6}
SEND_ORDER = [5, 0, 1, 6, 2, 7, 3, 4]
ARRIVE_ORDER = [0, 1, 2, 5, 3, 6, 4, 7]
BK = 7
BWIN, RWIN = [0, 1, 2, 3], [4, 5, 6, 7]
NST = 4
BUILDERS = [(True, 0, 28), (True, 1, 28), (True, 2, 28),
            (True, 4, 24), (True, 5, 24), (True, 6, 24),
            (False, 2, 28), (False, 3, 24), (False, 6, 24), (False, 7, 24)]

SCRATCH = {
    "zs": ("sbuf", [128, 1092], "float32"),
    "gs": ("sbuf", [128, 1024], "float32"),
    "land": ("sbuf", [128, NR * LW], "float32"),
    "mix": ("sbuf", [128, 1024], "float32"),
    "zt": ("sbuf", [128, 1024], "float32"),
    "S": ("sbuf", [128, 1024], "float32"),
    "H": ("sbuf", [128, 1024], "float32"),
    "prod": ("sbuf", [128, 1024], "float32"),
    "ysb": ("sbuf", [128, 512], "float32"),
    "ida": ("sbuf", [128, 129], "float32"),
    "idb": ("sbuf", [128, 129], "float32"),
    "dmat": ("sbuf", [128, 128], "float32"),
    "eye": ("sbuf", [128, 128], "float32"),
    "d_ia": ("dram", [129, 128], "float32"),
    "d_ib": ("dram", [129, 128], "float32"),
    "p1": ("psum", [128, 2048], "float32"),
    "p2": ("psum", [128, 2048], "float32"),
}
SEMAPHORES = (["zla", "zlb", "gla", "glb", "idm", "id1", "id2", "iem", "ie1", "ie2", "sent", "rel", "bz", "built",
               "mixed", "t1d", "evd", "t2d", "mud", "addd", "stored", "gfw", "yarr0", "yarr1"]
              + ["arr%d" % e for e in range(NR)] + ["sS%d" % s for s in range(NST)])

_CACHE = {}


def plan(route):
    if "p" in _CACHE:
        return _CACHE["p"]
    slots = [[[] for _ in range(NR)] for _ in range(NR)]
    for r in range(NR):
        for t in range(NT):
            for k in range(KK):
                slots[r][route[r][t][k]].append(t * KK + k)
    cnt = [[len(slots[r][e]) for r in range(NR)] for e in range(NR)]
    hc = [[len([j for j in slots[r][e] if j < 4 * WJ]) for r in range(NR)] for e in range(NR)]
    off = [[sum(cnt[e][:r]) for r in range(NR)] for e in range(NR)]
    pieces = [[[] for _ in range(NR)] for _ in range(NR)]
    src = [[0] * (NT * KK) for _ in range(NR)]
    for r in range(NR):
        fill = [0] * NW
        for e in range(NR):
            js = slots[r][e]
            for w in range(NW):
                idx = [i for i, j in enumerate(js) if j // WJ == w]
                if not idx:
                    continue
                pieces[r][e].append((w, idx[0], len(idx), fill[w]))
                for i in idx:
                    src[r][js[i]] = fill[w] + i - idx[0]
                fill[w] += len(idx)
    _CACHE["p"] = (cnt, off, hc, pieces, src)
    return _CACHE["p"]


def col_of(u):
    st, x = divmod(u, 2 * WJ)
    return (st if x < WJ else st + 4) * WJ + x % WJ


def chunks(own, k):
    out = []
    for st in range(NST):
        a = st * 2 * WJ
        for (o, hk, n) in BUILDERS:
            if o == own and hk == k:
                out.append((a, a + n))
            a += n
    return out


def parts(ua, ub):
    out, x = [], ua
    while x < ub:
        e = min(ub, (x // WJ + 1) * WJ)
        out.append((x, e, BK if col_of(x) // WJ in BWIN else 3))
        x = e
    return out


def s_incoming(k, st):
    tot = 0
    for (o, hk, _n) in BUILDERS:
        ua, ub = chunks(o, hk)[st]
        for (_a, _b, dk) in parts(ua, ub):
            if dk == k:
                tot += 16 if o else 8
    return tot


def band(v, q, sb, dram, out, s_m, s_1, s_2, last):
    v.memset(sb[:, 1:128], 0.0).then_inc(s_m, 1)
    v.memset(sb[:, 0:1], 1.0).then_inc(s_m, 1)
    v.memset(sb[:, 128:129], last).then_inc(s_m, 1)
    q.wait_ge(s_m, 3)
    q.dma_start(dram[:], sb[:]).then_inc(s_1, 16)
    q.wait_ge(s_1, 16)
    q.dma_start(out[:], dram[0:128, :]).then_inc(s_2, 16)


def build_S(g, T, topo, core, src_r, chs):
    v, pe, sem = g.vector, g.tensor, T.sem
    band(v, g.sync, T.ida, T.d_ia, T.dmat, sem.idm, sem.id1, sem.id2, -1.0)
    for (a, b) in chs:
        v.memset(T.H[:, a:b], 0.0).then_inc(sem.bz, 1)
    v.wait_ge(sem.bz, len(chs))
    pe.wait_ge(sem.id2, 16)

    def evac(st):
        a, b = chs[st]
        v.wait_ge(sem.t1d, st + 1)
        v.tensor_copy(T.S[:, a:b], T.p1[:, st * 512:st * 512 + b - a]).then_inc(sem.evd, 1)

    done = 0
    for st, (a, b) in enumerate(chs):
        for i, u in enumerate(range(a, b)):
            if st > 0 and i == 8:
                evac(st - 1)
            v.memset(T.H[0:src_r[col_of(u)] + 1, u:u + 1], 1.0).then_inc(sem.built, 1)
        done += b - a
        pe.wait_ge(sem.built, done)
        pe.matmul(T.p1[:, st * 512:st * 512 + b - a], T.dmat[:], T.H[:, a:b], True, True).then_inc(sem.t1d, 1)
    evac(len(chs) - 1)
    sent = 0
    rchip = (core // 8) | 1
    for st, (a, b) in enumerate(chs):
        g.wait_ge(sem.evd, st + 1)
        for (pa, pb, dk) in parts(a, b):
            dc = rchip * 8 + dk
            rid, pid, _s = topo.addr(dc)
            m = topo.mask(core, dc)
            ja = col_of(pa)
            g.remote_dma(T.S[:, ja:ja + pb - pa], T.S[:, pa:pb], sem["sS%d" % st], sem.sent, pid, rid, m)
            sent += 16 if m == 0xFFFF else 8
    return sent


def worker(g, T, r, wins, k, own_buf, own_base, own_sem, own_val, g_sem, g_val, pieces):
    sem = T.sem
    v, pe = g.vector, g.tensor
    nmix = 0
    need = {}
    for d in ARRIVE_ORDER:
        e = (r - d) % NR
        if d == 0:
            v.wait_ge(own_sem, own_val)
            buf, base = own_buf, own_base
        else:
            v.wait_ge(sem["arr%d" % e], 8)
            buf, base = T.land, e * LW
        for (w, cs, n, po) in pieces[r][e]:
            if w in wins:
                v.tensor_copy(T.mix[:, w * WJ + po:w * WJ + po + n],
                              buf[:, base + cs:base + cs + n]).then_inc(sem.mixed, 1)
                nmix += 1
                need[w] = nmix

    def win(buf, w):
        return buf[:, w * WJ:(w + 1) * WJ]

    def bank(buf, i):
        return buf[:, i * 512:i * 512 + WJ]

    def t1(i):
        pe.wait_ge(sem.mixed, need[wins[i]])
        pe.matmul(bank(T.p1, i), win(T.mix, wins[i]), T.eye[:], True, True).then_inc(sem.t1d, 1)

    def t2(i):
        pe.wait_ge(sem.evd, i + 1)
        pe.wait_ge(sem["sS%d" % i], s_incoming(k, i))
        pe.matmul(bank(T.p2, i), win(T.zt, wins[i]), win(T.S, wins[i]), True, True).then_inc(sem.t2d, 1)

    pe.wait_ge(sem.ie2, 16)
    t1(0), t1(1), t2(0), t1(2), t2(1), t1(3), t2(2), t2(3)

    def evac(i):
        v.wait_ge(sem.t1d, i + 1)
        v.tensor_copy(win(T.zt, wins[i]), bank(T.p1, i)).then_inc(sem.evd, 1)

    def mult(i):
        v.wait_ge(sem.t2d, i + 1)
        v.tensor_tensor(win(T.prod, wins[i]), bank(T.p2, i), win(T.gs, wins[i]), AluOpType.mult).then_inc(sem.mud, 1)

    def add(i):
        w = wins[i]
        v.wait_ge(sem.mud, i + 1)
        v.tensor_tensor(T.ysb[:, w * WT:(w + 1) * WT], T.prod[:, w * WJ:(w + 1) * WJ:2],
                        T.prod[:, w * WJ + 1:(w + 1) * WJ:2], AluOpType.add).then_inc(sem.addd, 1)

    evac(0), evac(1)
    v.wait_ge(g_sem, g_val)
    mult(0), evac(2), add(0), mult(1), evac(3), add(1), mult(2), add(2), mult(3), add(3)


def helper_program(g, core, T, topo):
    cnt, off, hc, pieces, src = plan(T.tables["ROUTE"])
    sem = T.sem
    ch, k = core // 8, core % 8
    own = (ch % 2 == 1)
    rcore = (ch | 1) * 8 + 3
    r = T.rank_of(rcore)
    if r is None:
        return
    sent = 0
    if own and k == BK:
        band(g.vector, g.scalar, T.idb, T.d_ib, T.eye, sem.iem, sem.ie1, sem.ie2, 0.0)
        worker(g, T, r, BWIN, BK, T.land, r * LW, sem["arr%d" % r], 8, sem.gfw, 16, pieces)
        rid, pid, _s = topo.addr(rcore)
        for i in (0, 1):
            g.wait_ge(sem.addd, 2 * i + 2)
            g.remote_dma(T.ysb[:, i * WJ:(i + 1) * WJ], T.ysb[:, i * WJ:(i + 1) * WJ], sem["yarr%d" % i], sem.sent,
                         pid, rid, 0xFFFF)
            sent += 16
    if own:
        for d, hk in RELAY.items():
            if hk == k:
                dst = (r + d) % NR
                n, h = cnt[r][dst], hc[r][dst]
                g.wait_ge(sem.rel, 8)
                for (a, b, dc) in ((0, h, (T.cores[dst] // 8) * 8 + BK), (h, n, T.cores[dst])):
                    rid, pid, _s = topo.addr(dc)
                    g.remote_dma(T.land[:, r * LW + a:r * LW + b], T.land[:, a:b], sem["arr%d" % r], sem.sent,
                                 pid, rid, 0x00FF)
                    sent += 8
    chs = chunks(own, k)
    if chs:
        sent += build_S(g, T, topo, core, src[r], chs)
    if sent:
        g.wait_ge(sem.sent, sent)


def rank_program(g, core, T, topo):
    r = T.rank_of(core)
    if r is None:
        helper_program(g, core, T, topo)
        return
    cnt, off, hc, pieces, src = plan(T.tables["ROUTE"])
    sem = T.sem
    v, sy, sc = g.vector, g.sync, g.scalar
    tot = off[r][NR - 1] + cnt[r][NR - 1]
    half = off[r][4]
    chip0 = (core // 8) * 8

    sy.dma_start(T.zs[:, 0:half], T.z[:, 0:half]).then_inc(sem.zla, 16)
    sc.dma_start(T.zs[:, half:tot], T.z[:, half:tot]).then_inc(sem.zlb, 16)
    sy.dma_start(T.gs[:, 0:512], T.g[:, 0:512]).then_inc(sem.gla, 16)
    sc.dma_start(T.gs[:, 512:1024], T.g[:, 512:1024]).then_inc(sem.glb, 16)
    band(v, sc, T.idb, T.d_ib, T.eye, sem.iem, sem.ie1, sem.ie2, 0.0)

    waited = set()
    sent = 0
    for d in SEND_ORDER:
        dst = (r + d) % NR
        zl = "zla" if dst < 4 else "zlb"
        if zl not in waited:
            g.wait_ge(sem[zl], 16)
            waited.add(zl)
        n, h, o = cnt[r][dst], hc[r][dst], off[r][dst]
        if d == 0:
            todo = [(0, h, r * LW, chip0 + BK, sem["arr%d" % r], 0xFF00)]
        elif d in RELAY:
            todo = [(0, n, 0, chip0 + RELAY[d], sem.rel, 0xFF00)]
        else:
            todo = [(0, h, r * LW, (T.cores[dst] // 8) * 8 + BK, sem["arr%d" % r], 0x00FF),
                    (h, n, r * LW, T.cores[dst], sem["arr%d" % r], 0x00FF)]
        for (a, b, base, dc, rs, m) in todo:
            rid, pid, _s = topo.addr(dc)
            g.remote_dma(T.land[:, base + a:base + b], T.zs[:, o + a:o + b], rs, sem.sent, pid, rid, m)
            sent += 8
    for zl in ("zla", "zlb"):
        if zl not in waited:
            g.wait_ge(sem[zl], 16)
    g.wait_ge(sem.gla, 16)
    rid, pid, _s = topo.addr(chip0 + BK)
    g.remote_dma(T.gs[:, 0:512], T.gs[:, 0:512], sem.gfw, sem.sent, pid, rid, 0xFFFF)
    sent += 16
    g.wait_ge(sem.sent, sent)

    worker(g, T, r, RWIN, 3, T.zs, off[r][r], sem["zla" if r < 4 else "zlb"], 16, sem.glb, 16, pieces)

    for i in (0, 1):
        sy.wait_ge(sem["yarr%d" % i], 16)
        sy.dma_start(T.y[:, i * WJ:(i + 1) * WJ], T.ysb[:, i * WJ:(i + 1) * WJ]).then_inc(sem.stored, 16)
        sc.wait_ge(sem.addd, 2 * i + 2)
        sc.dma_start(T.y[:, (i + 2) * WJ:(i + 3) * WJ], T.ysb[:, (i + 2) * WJ:(i + 3) * WJ]).then_inc(sem.stored, 16)
    sy.wait_ge(sem.stored, 64)
